import numpy as np, ml_dtypes
CORES = [8,9,10,11,12,13]
N = 6
BF = ml_dtypes.bfloat16
def gentries(a):
    return np.ascontiguousarray(a.reshape(8, 16, -1).transpose(0, 2, 1)).reshape(8, -1)
def gtable(e):
    e = np.asarray(e); return np.ascontiguousarray(e.reshape(8, -1, 16).transpose(0, 2, 1)).reshape(128, -1).astype(np.int32)
V, WN, M, S, RO, LIM, PEN, T0 = 4096, 1024, 384, 3, 2, 20, 45, 34816
H = WN // 2
def parts(rng):
    return rng.integers(0, 256, (N, 8, 16, V)), rng.integers(0, V, (N, 8, 16, WN)), rng.integers(0, V, (N, 8, M)), rng.integers(0, 256, (N, 8, 16, M))
def pack(X, O, v, z):
    return {"tracks": np.ascontiguousarray(X.reshape(N, 128, V)).astype(np.float32).astype(BF),
            "nb": np.ascontiguousarray((O[..., :H] + V * O[..., H:]).reshape(N, 128, H)).astype(np.int32),
            "v": np.stack([gtable(a) for a in v]), "z": np.ascontiguousarray(z.reshape(N, 128, M)).astype(np.float32).astype(BF)}
def bits(b):
    return 255 * ((np.asarray(b)[..., None] >> (15 - np.arange(16))) & 1)
def tune(b, goal):
    t = bits(b); t = t - LIM * (t > 0); need = int((goal - np.add.reduce((2 * np.arange(16) + 1) * t)) % V)
    for p in range(15, -1, -1):
        d = min(LIM, need // (2 * p + 1)); t[p] += d; need -= d * (2 * p + 1)
    return t
def ladder(z):
    t = np.tile(np.where(np.abs(z - 128) > 64, 128, 0), (3, 1)); t[:, 0] = z[0]
    for j in (1, 2, 3): t[j - 1, 4 - j] = z[4 - j] + (LIM + j) * (1 if z[4 - j] < 128 else -1)
    return t
def setup_inputs(rng):
    X, O, v, z = parts(rng)
    few = np.take_along_axis(rng.integers(0, V, (N, 8, 16)), rng.integers(0, 16, (N, 8, M)), 2)
    return pack(X, O, np.where(rng.random((N, 8, M)) < 0.25, few, v), z)
def uneven(rng, n):
    a = np.minimum((np.exp2(8 * rng.random((N, 8, 1, n))) * rng.random((N, 8, 16, n))).astype(np.int64), 255)
    return np.where(rng.random(a.shape) < 0.5, 255 - a, a)
def setup_inputs_spread(rng):
    O = np.minimum((V * rng.random((N, 8, 16, WN)) ** 3).astype(np.int64), V - 1); v = np.minimum((V * rng.random((N, 8, M)) ** 2).astype(np.int64), V - 1)
    return pack(uneven(rng, V), O, v, uneven(rng, M))
def setup_inputs_ends(rng):
    X, O, v, z = parts(rng)
    X = 255 * rng.integers(0, 2, X.shape); z = 255 * rng.integers(0, 2, z.shape)
    e = (V - 1) * rng.integers(0, 2, (N, 8, 16, H)); keep = rng.random((N, 8, 16, H)) < 0.75
    keep[..., 0] = True; keep[..., H - 1] = True; e[:, :, 14, H - 1] = V - 1; e[:, :, 15, H - 1] = 0; e[:, :, 14, 0] = 0; e[:, :, 15, 0] = V - 1
    O = np.concatenate([np.where(keep, e, O[..., :H]), np.where(keep, e, O[..., H:])], axis=3)
    v = np.where(rng.random(v.shape) < 0.75, (V - 1) * rng.integers(0, 2, v.shape), v)
    X[:, 1::2, :, V - 1] = X[:, 1::2, :, 0]
    z[..., M // 2:M // 2 + 8] = 255
    v[:, :, M - 2:] = V - 1; z[..., M - 1] = X[..., V - 1]; z[..., M - 2] = 255 - X[..., V - 1]
    v[:, :, :2] = 0; z[..., 0] = X[..., 0]; z[..., 1] = 255 - X[..., 0]
    return pack(X, O, v, z)
def setup_inputs_ties(rng):
    X, O, v, z = parts(rng)
    B = np.broadcast_to(rng.integers(60, 196, (1, 8, 16, 6)), (N, 8, 16, 6)); jog = np.array([LIM, LIM + 1, LIM + 2, LIM + 3, LIM + 4, -LIM, -LIM - 1, -LIM - 2])
    X = np.take_along_axis(B, np.broadcast_to(rng.integers(0, 6, (N, 8, 1, V)), X.shape), 3)
    X = np.where((rng.random((N, 8, 1, V)) < 0.5) & (rng.random(X.shape) < 0.15), X + rng.choice(jog, X.shape), X)
    z = np.take_along_axis(B, np.broadcast_to(rng.integers(0, 6, (N, 8, 1, M)), z.shape), 3)
    z = np.where(rng.random(z.shape) < 0.3, z + rng.choice(jog, z.shape), z)
    O[:, ::2] = np.tile(O[:, ::2, :4], (1, 1, 4, 1))
    return pack(X, O, v, z)
def calm(rng, X, O, v, z, g, low):
    for r in range(N):
        t = rng.integers(0, 256, 16); B = rng.permutation(V)[:5]; f, n, L = int(B[0]), int(B[1]), B[2:]
        w = rng.permutation(np.setdiff1d(np.arange(WN), np.array([f & (WN - 1)])))[:2]; go, end = int(w[0]), int(w[1])
        X[r, g][:, f] = t; X[r, g][:, n] = np.where(np.abs(t - 128) > 64, 128, 0); X[r, g][:, L] = ladder(t).T
        O[r, g][:, go] = f; O[r, g][:, end] = n; O[r, g][:, f & (WN - 1)] = L[rng.permutation(16) % 3]
        stay = np.ones(M, bool); z[r, g] = t[:, None]
        if r in low: stay = np.isin(np.arange(M), rng.permutation(M)[:low[r]])
        else: z[r, g][1:] = rng.integers(0, 256, (15, M))
        v[r, g] = np.where(stay, end, go) + WN * rng.integers(0, V // WN, M)
def setup_inputs_corners(rng):
    X, O, v, z = parts(rng); C = min(M // 4, WN // (4 * N)); own = 1 + np.arange(3 * N * C).reshape(N, 3, C); top = 3 * N * C + 1
    O[..., 0] = rng.choice(np.array([0, V - 1]), (N, 8, 16)); O[..., WN - 1] = rng.choice(np.array([0, V - 1]), (N, 8, 16))
    for r in range(N):
        for g in range(8):
            o = rng.permutation(M); rest = o[3 * C:]
            v[r, g, rest[::2]] = rng.choice(np.array([0, V - 1]), len(rest[::2]))
            for j in range(3):
                E = own[r, j]; ln = o[j * C:(j + 1) * C]; b = rng.integers(0, 65536, C); d = rng.integers(1, 1000, C)
                v[r, g, ln] = E + WN * rng.integers(0, V // WN, C); z[r, g][:, ln] = bits(b).T
                for s in range((S, 1, 2)[j]):
                    q = (r + s) % N
                    t = 65535 - (S - 1 - s) * d if j == 0 else np.full(C, T0 + j - 1)
                    b = b ^ (65535 - t); X[q, g][:, E] = bits(b).T
                    if j == 0:
                        O[q, g][:, E] = rng.integers(top, V, (16, C)); O[q, g][rng.integers(0, 16, C), E] = E
                    else: O[q, g][:, E] = E
    two = rng.permutation(8)[:2]; few = rng.permutation(4)
    for i in range(2): calm(rng, X, O, v, z, int(two[i]), {(i + 2 * j) % N: int(few[(i * (N // 2) + j) % 4]) for j in range(N // 2)})
    return pack(X, O, v, z)
def apart(rng, X, O, v, z, g, q, b):
    K = (S - 1) * M; E = rng.permutation(WN - 1)[:K]; E[K - 1] = WN - 1
    B = E + WN * rng.integers(0, V // WN, K); B[K - 1] = V - 1; B2 = (B[:M] + WN) % V
    left = int(np.setdiff1d(np.arange(WN), E)[0]); X[:, g, :, left] = 128
    for r in range(N):
        k = rng.integers(0, 16, K); k[K - 1] = 15
        X[r, g][:, B] = bits(int(b[r]))[:, None]; O[r, g][:, E] = left; O[r, g][k, E] = B
        if r == q:
            X[r, g][:, B2] = bits(65535 - int(b[q]))[:, None]; O[r, g][(k[:M] + 1 + rng.integers(0, 15, M)) % 16, E[:M]] = B2
    for s in range(1, S):
        r = (q - s) % N; v[r, g] = B[(s - 1) * M:s * M]
        for i in range(M): z[r, g, :, i] = tune(int(b[r]) ^ (65534 - T0), int(rng.integers(1, V)))
    v[q, g] = B2; z[q, g] = bits(65535 - int(b[q]))[:, None]
def setup_inputs_crowd(rng):
    X, O, v, z = parts(rng)
    v = np.take_along_axis(rng.integers(0, V, (N, 8, 3)), rng.integers(0, 3, (N, 8, M)), 2)
    o = rng.permutation(8)
    for i in range(7):
        g = int(o[i]); q = int(rng.integers(0, N)); a = int((V - 1, 0, WN, rng.integers(1, V - 1), V - 1, rng.integers(1, V - 1), 0)[i]); first = q - S + (2 if i < 2 else 1)
        t = np.sort(T0 + 2 + rng.permutation(65534 - T0)[:S - 1]); b = rng.integers(0, 65536, N)
        if i in (2, 3): t[S - 2] = t[S - 3]
        if i >= 4: t[S - 2] = 65535
        for j in range(1, S): b[(first + j) % N] = b[(first + j - 1) % N] ^ (65535 - int(t[j - 1]))
        b = b ^ (int(b[q]) ^ int(rng.integers(1, 65535)))
        if i == 6:
            apart(rng, X, O, v, z, g, q, b); continue
        for r in range(N): X[r, g, :, a] = bits(int(b[r]))
        O[:, g, :, a & (WN - 1)] = a
        if i == 0: X[:, g, :, 0] = 128; O[:, g, :15, a & (WN - 1)] = 0
        v[:, g] = (a + WN * rng.integers(0, V // WN, (N, M))) % V
        for r in range(N):
            m = T0 + 1
            if i in (2, 3) and r == q: m = T0
            if i in (2, 3) and r == (q - 1) % N: m = int(t[S - 2])
            if i >= 4 and r == q: m = 65535
            z[r, g] = tune(int(b[r]) ^ (65535 - m), V - 1)[:, None]
        if i in (2, 3):
            e = (a + 1 + np.arange(3)) % V
            X[q, g][:, e] = ladder(z[q, g, :, 0]).T; O[q, g, :, (a - 1) & (WN - 1)] = e[rng.permutation(16) % 3]
        if i == 2:
            y = tune(int(b[q]) ^ (65535 - T0), V - 2); z[q, g, :, 1::2] = y[:, None]
            f = (a + 4) % V; nx = (q + 1) % N; x = np.full(16, 128); x[[0, 4, 15]] = y[[0, 4, 15]]
            X[q, g, :, f] = x; O[q, g, :, (a - 2) & (WN - 1)] = f
            X[nx, g][:, e] = ladder(x).T; O[nx, g, :, f & (WN - 1)] = e[rng.permutation(16) % 3]
        if i == 1: z[q, g, :, M - 1] = bits(65535 - int(b[q]))
        if i == 3: z[q, g, :, M - 1] = bits(int(b[q]))
        if i == 5: z[q, g, :, M - max(1, S * M - 1024):] = bits(65535 - int(b[q]))[:, None]
    return pack(X, O, v, z)
def check_inputs(d):
    bad = []
    for k, hi in (("tracks", 255), ("nb", V * V - 1), ("v", V - 1), ("z", 255)):
        a = np.asarray(d[k]).astype(np.float64)
        if not np.all((a >= 0) & (a <= hi) & (a == np.floor(a))): bad.append("range of " + k)
    return bad
def reference(tracks, nb, v, z):
    X = np.ascontiguousarray(tracks.astype(np.float32).astype(np.int16).reshape(N, 8, 16, V).transpose(0, 1, 3, 2))
    a = nb.astype(np.int64).reshape(N, 8, 16, H)
    O = np.ascontiguousarray(np.concatenate([a & (V - 1), a // V], axis=3).transpose(0, 1, 3, 2))
    bo = np.stack([gentries(e) for e in v]).astype(np.int64)
    tr = np.ascontiguousarray(z.astype(np.float32).astype(np.int16).reshape(N, 8, 16, M).transpose(0, 1, 3, 2))
    r = np.arange(N)[:, None, None]; g = np.arange(8)[None, :, None]
    two = (1 << (15 - np.arange(16))).astype(np.int32); odd = 2 * np.arange(16) + 1
    settled = np.zeros((N, 8), np.int64)
    for rnd in range(RO):
        u = np.add.reduce(tr * odd, axis=-1) & (V - 1)
        vs, zs, mark, live, c, trail = bo, tr, np.full((N, 8, M), T0), np.ones((N, 8, M), bool), np.zeros((N, 8, M), np.int64), []
        for s in range(S):
            q = (r + s) % N; w = vs & (WN - 1)
            P = O[q, g, w]
            x = X[q[..., None], g[..., None], P]
            near = np.abs(x - zs[:, :, :, None, :]) <= LIM + (settled[q, g] & 3)[..., None, None]
            T = np.add.reduce(np.where(near, two, 0), axis=-1)
            k = np.argmax(T, axis=-1); best = np.max(T, axis=-1)
            go = live & (best > mark)
            nv = np.take_along_axis(P, k[..., None], 3)[..., 0]; nz = np.take_along_axis(x, k[..., None, None], 3)[:, :, :, 0]
            trail.append((w, k, nv))
            vs = np.where(go, nv, vs); zs = np.where(go[..., None], nz, zs); mark = np.where(go, best, mark); c = c + go; live = go
            if s == 0: z1 = zs
        hit = np.zeros((N, 8, V), bool); more = np.zeros((N, 8, WN, 16), np.int64); settled = np.zeros((N, 8), np.int64)
        G = np.broadcast_to(g, (N, 8, M))
        for s in range(S):
            w, k, nv = trail[s]; Q = np.broadcast_to((r + s) % N, (N, 8, M))
            e = c == s + 1; hit[Q[e], G[e], nv[e]] = True
            e = c > s + 1; np.add.at(more, (Q[e], G[e], w[e], k[e]), u[e])
            e = (c == s) if s < S - 1 else (c >= s)
            settled = settled + np.roll(np.add.reduce(e.astype(np.int64), axis=2), s, axis=0)
        X = np.where(hit[..., None], np.maximum(X - PEN, 0), X).astype(np.int16); O = (O + more) & (V - 1)
        bo = np.where(c > 0, vs, (bo + u) & (V - 1)); tr = np.where((c > 0)[..., None], (tr + z1) >> 1, tr).astype(np.int16)
    o = O.transpose(0, 1, 3, 2)
    return {"yx": np.ascontiguousarray(X.transpose(0, 1, 3, 2)).reshape(N, 128, V).astype(np.float32).astype(BF),
            "yn": np.ascontiguousarray(o[..., :H] + V * o[..., H:]).reshape(N, 128, H).astype(np.float32),
            "yv": np.stack([gtable(e) for e in bo]).astype(np.float32),
            "yz": np.ascontiguousarray(tr.transpose(0, 1, 3, 2)).reshape(N, 128, M).astype(np.float32).astype(BF)}

@@ -1,0 +1,469 @@
+from concourse.mybir import dt, AluOpType as OP, ActivationFunctionType as AF, AxisListType
+
+RO, ST, NCH = 2, 3, 3
+BS = {"float32": 4, "int32": 4, "bfloat16": 2, "float16": 2, "uint16": 2}
+SCRATCH, ALIAS, POOL = {}, {}, {}
+
+
+def _b(names, cols, dtype, where="sbuf"):
+    for n in names.split():
+        SCRATCH[n] = (where, [128, cols], dtype)
+
+
+def _s(names, cols, dtype):
+    for n in names.split():
+        w = 32 // BS[dtype]; o = POOL.get(dtype, 0)
+        ALIAS[n] = ("pool_" + dtype, o, cols); POOL[dtype] = o + (cols + w - 1) // w * w
+
+
+_b("X", 4112, "bfloat16"); _b("O OX OT", 1024, "int32"); _b("NB", 512, "int32"); _b("YN EXS", 512, "float32")
+_b("XG0 XG1 XG2 NR0 NR1", 2048, "bfloat16"); _b("PO0 PO1 PO2 PO3", 128, "uint16"); _b("PF0 PF1 PF2 PF3 SEL0 SEL1 M0 IOH", 128, "float16")
+_b("D0 D1 D2 KEY MI EX0 EX1 PEN", 512, "float32", "psum"); _b("NO0 NO1", 128, "bfloat16")
+_b("S1_0 S1_1 S1_2", 384, "float32"); _b("SG0 SG1 SG2", 24 * 34, "bfloat16"); _b("XOH0 XOH1 YU", 24 * 128, "float16"); _b("HOH", 24 * 128, "bfloat16")
+_s("VMB0 VMB1 VMB2 QB0 QB1 QB2 LOB0 LOB1 LOB2 HP0 HP1 HP2 XC0 XC1 WL0 WL1 FA FB FC BA BB BC BD EF EG EH TF HM0 HM1 HM2 FC0 FC1 UM0 UM1 CF", 24, "float32")
+_s("VL IA IB IC LWI OA OB EA EB EC PA PB_ PC", 24, "int32"); _s("LW", 24, "uint16"); _s("NF MM PB I16", 8, "float32"); _s("QA QT", 24, "bfloat16")
+for _r in range(RO):
+    for _i in range(3):
+        _b("Z%d_%d" % (_r, _i), 384, "bfloat16")
+        _s("GO%d_%d" % (_r, _i), 24, "float32"); _s("LU%d_%d" % (_r, _i), 24, "uint16")
+        if _i < 2:
+            _s("F%d_%d" % (_r, _i), 48, "float32"); _b("ZO%d_%d" % (_r, _i), 384, "bfloat16")
+        if _i > 0:
+            _s("FL%d_%d" % (_r, _i), 48, "float32"); _s("GL%d_%d" % (_r, _i), 24, "float32"); _s("LL%d_%d" % (_r, _i), 24, "uint16")
+    _s("UV%d UL%d" % (_r, _r), 48, "float32")
+_b("HC0", 264, "float32"); _b("HC", 264, "bfloat16"); _b("HS", 4096, "bfloat16")
+_b("RY", 384, "float32"); _b("RB RN RE RD ONE", 384, "bfloat16")
+_b("IOT", 144, "float32"); _b("IOB ID HID NID FI NFI REP NREP KB QROW", 128, "bfloat16"); _s("CI", 8, "int32")
+_s("W8 WU B8B", 8, "bfloat16"); _s("B8", 8, "float16"); _s("BM", 16, "float16"); _b("DB", 144, "float16"); _b("DUB", 144, "bfloat16")
+_b("RST KF GF", 128, "float32"); _b("ZR", 512, "float16")
+_s("AL", 48, "float32"); _s("AR FCOL", 1, "float32"); _s("AC AB", 1, "bfloat16"); _s("AI AJ", 1, "int32")
+for _d in POOL:
+    _b("pool_" + _d, POOL[_d], _d)
+
+SEMAPHORES = ["V", "S", "P", "G", "ls", "dnb", "dv", "dz", "dx0", "dx1", "dx2", "dx3", "dhs", "dex", "dox", "oyx0", "oyx1", "oyn", "oyv"]
+for _r in range(RO):
+    for _j in (1, 2):
+        for _i in range(NCH):
+            SEMAPHORES += ["aF%d_%d_%d" % (_r, _j, _i), "aZ%d_%d_%d" % (_r, _j, _i)]
+        SEMAPHORES += ["aG%d_%d" % (_r, _j), "aL%d_%d" % (_r, _j)]
+    SEMAPHORES += ["aU%d" % _r]
+
+MAG = 12582912.0
+M16 = 201326592.0
+THR0 = 16.0 * (34816 + 1) - 0.5
+
+
+def rank_program(g, core, T, topo):
+    rank = T.rank_of(core)
+    if rank is None:
+        return
+    N = len(T.cores)
+    nxt, prv = T.cores[(rank + 1) % N], T.cores[(rank - 1) % N]
+    eng = {"V": g.vector, "S": g.scalar, "P": g.tensor, "G": g, "Y": g.sync}
+    cnt, snap, acc, known = {}, {}, {}, {q: {} for q in eng}
+
+    def A(name, c0=0, c1=None, step=1, p0=0, p1=128):
+        if name in ALIAS:
+            n, o, w = ALIAS[name]
+            return (n, o + c0, o + (w if c1 is None else c1), step, p0, p1)
+        return (name, c0, SCRATCH[name][1][1] if c1 is None else c1, step, p0, p1)
+
+    def ap(a):
+        t = T[a[0]]
+        return t[a[4]:a[5], a[1]:a[2]] if a[3] == 1 else t[a[4]:a[5], a[1]:a[2]:a[3]]
+
+    def span(a):
+        w = BS[SCRATCH[a[0]][2]]
+        if SCRATCH[a[0]][0] == "psum": return (0, 128, 0, 2048)
+        return (a[4], a[5], a[1] * w // 16 * 16, (a[2] * w + 15) // 16 * 16)
+
+    def learn(q, comp, n):
+        k = known[q]
+        if k.get(comp, 0) >= n: return
+        k[comp] = n
+        for c2, n2 in snap.get((comp, n), {}).items():
+            if k.get(c2, 0) < n2: k[c2] = n2
+
+    def hazards(q, comp, reads, writes):
+        need = {}
+        for lst, w in ((reads, False), (writes, True)):
+            for a in lst:
+                ps = SCRATCH[a[0]][0] == "psum"; s = span(a)
+                for (t, ow, oc, on, oq) in acc.get(a[0], []):
+                    if not (s[0] < t[1] and t[0] < s[1] and s[2] < t[3] and t[2] < s[3]): continue
+                    if ps:
+                        if oq == q and oc == comp and (q == "P" or not (ow or w)): continue
+                    elif not (ow or w): continue
+                    if oc[0] in "do" and known[q].get(oc, 0) < on: on = cnt[oc]
+                    if need.get(oc, 0) < on: need[oc] = on
+        for oc in sorted(need, key=lambda c: -need[c]):
+            if known[q].get(oc, 0) < need[oc]:
+                eng[q].wait_ge(T.sem[oc], need[oc]); learn(q, oc, need[oc])
+
+    def note(q, comp, n, reads, writes):
+        for a in writes:
+            s = span(a); ps = SCRATCH[a[0]][0] == "psum"
+            if not ps: acc[a[0]] = [r for r in acc.get(a[0], []) if not (s[0] <= r[0][0] and r[0][1] <= s[1] and s[2] <= r[0][2] and r[0][3] <= s[3])]
+        for lst, w in ((reads, False), (writes, True)):
+            for a in lst:
+                s = span(a)
+                l = [r for r in acc.setdefault(a[0], []) if not (r[0] == s and r[1] == w and r[2] == comp and r[4] == q)]
+                acc[a[0]] = l + [(s, w, comp, n, q)]
+
+    def run(q, reads, writes, call):
+        hazards(q, q, reads, writes)
+        i = call(); cnt[q] = cnt.get(q, 0) + 1
+        i.then_inc(T.sem[q], 1)
+        snap[(q, cnt[q])] = dict(known[q])
+        note(q, q, cnt[q], reads, writes)
+
+    def dma(sem, out, in_, q="Y", reads=(), writes=()):
+        hazards(q, sem, reads, writes)
+        eng[q].dma_start(out, in_).then_inc(T.sem[sem], 16)
+        cnt[sem] = cnt.get(sem, 0) + 16
+        snap[(sem, cnt[sem])] = dict(known[q])
+        note(q, sem, cnt[sem], reads, writes)
+
+    def send(dst, out, in_, sem):
+        hazards("G", "ls", [in_], [])
+        rid, pid, _ = topo.addr(dst)
+        g.remote_dma(ap(out), ap(in_), T.sem[sem], T.sem["ls"], pid, rid, topo.mask(core, dst))
+        cnt["ls"] = cnt.get("ls", 0) + len(topo.engines(core, dst))
+
+    def arrives(sem, a, src):
+        cnt[sem] = len(topo.engines(src, core)); note("R", sem, cnt[sem], [], [a])
+
+    def col(x):
+        return (ap(x), [x]) if isinstance(x, tuple) else (x, [])
+
+    def ts(out, in0, s1, op0, s2=None, op1=None):
+        v1, r1 = col(s1); v2, r2 = col(s2)
+        if op1 is None: run("V", [in0] + r1, [out], lambda: g.vector.tensor_scalar(ap(out), ap(in0), v1, None, op0))
+        else: run("V", [in0] + r1 + r2, [out], lambda: g.vector.tensor_scalar(ap(out), ap(in0), v1, v2, op0, op1))
+
+    def tt(out, a, b, op):
+        run("V", [a, b], [out], lambda: g.vector.tensor_tensor(ap(out), ap(a), ap(b), op))
+
+    def cp(out, a):
+        run("V", [a], [out], lambda: g.vector.tensor_copy(ap(out), ap(a)))
+
+    def ms(out, c):
+        run("V", [], [out], lambda: g.vector.memset(ap(out), c))
+
+    def mm(out, l, r, start, stop):
+        run("P", [l, r], [out], lambda: g.tensor.matmul(ap(out), ap(l), ap(r), start, stop))
+
+    def act(out, a, f, bias=None):
+        v, r = col(bias)
+        if bias is None: run("S", [a], [out], lambda: g.scalar.activation(ap(out), ap(a), f))
+        else: run("S", [a] + r, [out], lambda: g.scalar.activation(ap(out), ap(a), f, bias=v))
+
+    def gather_v(out, win, off):
+        run("V", [win, off], [out], lambda: g.vector.tensor_copy(ap(out), ap(win).indirect(ap(off))))
+
+    def gather_s(out, win, off):
+        run("S", [win, off], [out], lambda: g.scalar.activation(ap(out), ap(win).indirect(ap(off)), AF.Copy))
+
+    def iota(out, pat, base, cm, flag=True):
+        if flag: run("G", [], [out], lambda: g.iota(ap(out), pat, base, cm, allow_small_or_imprecise_dtypes=True))
+        else: run("G", [], [out], lambda: g.iota(ap(out), pat, base, cm))
+
+    fq = []
+
+    def tick(k=1):
+        while fq and k: fq.pop(0)(); k -= 1
+
+    def weave(a, b):
+        o = []
+        for i in range(max(len(a), len(b))): o += a[i:i + 1] + b[i:i + 1]
+        return o
+
+    for r in range(RO):
+        for s in (1, 2):
+            for i in range(NCH):
+                arrives("aF%d_%d_%d" % (r, s, i), A("FL%d_%d" % (r, s), 16 * i, 16 * i + 16), prv)
+                arrives("aZ%d_%d_%d" % (r, s, i), A("Z%d_%d" % (r, s), 128 * i, 128 * i + 128), prv)
+            arrives("aG%d_%d" % (r, s), A("GL%d_%d" % (r, s)), nxt)
+            arrives("aL%d_%d" % (r, s), A("LL%d_%d" % (r, s)), T.cores[(rank + s) % N])
+        arrives("aU%d" % r, A("UL%d" % r), prv)
+
+    dma("dnb", ap(A("NB")), T.nb[:, :], "Y", [], [A("NB")])
+    dma("dv", ap(A("VL")), T.v[:, :], "S", [], [A("VL")])
+    for i in range(4):
+        a = A("X", 1024 * i, 1024 * i + 1024)
+        dma("dx%d" % i, ap(a), T.tracks[:, 1024 * i:1024 * i + 1024], "YS"[i % 2], [], [a])
+    dma("dz", ap(A("Z0_0")), T.z[:, :], "Y", [], [A("Z0_0")])
+    iota(A("CI", 0, 1), [[1, 1]], 0, 1, False)
+    iota(A("IOT"), [[1, 144]], 0, 0)
+    iota(A("I16"), [[16, 8]], 0, 0)
+    iota(A("KB", p1=1), [[0, 8], [-1, 16]], 15, 0)
+    iota(A("KF"), [[0, 8], [1, 16]], 0, 0)
+    iota(A("GF"), [[1, 8], [0, 16]], 0, 0)
+    ms(A("X", 4096, 4112), 512.0); ms(A("ONE"), 1.0); ms(A("QROW", p1=1), -0.25); ms(A("PB", 4, 5), 524288.0)
+    cp(A("CF", 0, 1), A("CI", 0, 1))
+    ts(A("CI", 4, 5), A("CI", 0, 1), 15, OP.bitwise_and); cp(A("CF", 4, 5), A("CI", 4, 5))
+    ts(A("ID"), A("IOT", 0, 128), A("CF", 0, 1), OP.is_equal)
+    tt(A("CF", 8, 9), A("CF", 0, 1), A("CF", 4, 5), OP.subtract)
+    ts(A("FI"), A("ID"), 1.5625 / 64, OP.mult); ts(A("NFI"), A("ID"), -1.5625 / 64, OP.mult)
+    ts(A("CF", 12, 13), A("CF", 8, 9), 15.0, OP.add)
+    ts(A("CF", 16, 17), A("CF", 4, 5), 2.0, OP.mult, 1.0, OP.add)
+    for b in range(4):
+        ts(A("CI", 1, 2), A("CI", 4, 5), b, OP.arith_shift_right, 1, OP.bitwise_and)
+        ts(A("PB", 0, 1), A("CI", 1, 2), 2.0 ** -(1 << b) - 1.0, OP.mult, 1.0, OP.add)
+        tt(A("PB", 4, 5), A("PB", 4, 5), A("PB", 0, 1), OP.mult)
+    ts(A("W8"), A("I16"), A("CF", 8, 9), OP.is_equal, A("PB", 4, 5), OP.mult)
+    ts(A("RST"), A("KF"), 0.0, OP.is_equal, -4194304.0, OP.mult)
+    ts(A("LWI"), A("VL"), 1023, OP.bitwise_and)
+    ts(A("B8"), A("I16"), A("CF", 8, 9), OP.is_equal)
+    cp(A("LW"), A("LWI"))
+    ts(A("BM"), A("IOT", 0, 16), A("CF", 4, 5), OP.is_equal)
+    ts(A("O", 0, 512), A("NB"), 4095, OP.bitwise_and)
+    ts(A("O", 512, 1024), A("NB"), 12, OP.arith_shift_right)
+
+    def og(n, r):
+        s, i = divmod(n, 3)
+        if s:
+            f = A("FL%d_%d" % (r, s), 16 * i, 16 * i + 8); c = (8 * i, 8 * i + 8)
+            ts(A("OA", *c), f, 2048.0, OP.add); tick(); ts(A("OB", *c), A("OA", *c), 1023, OP.bitwise_and); tick(); cp(A("LW", *c), A("OB", *c)); tick()
+        po = A("PO%d" % (n % 4))
+        gather_v(po, A("O"), A("LW", 8 * i, 8 * i + 8)); tick()
+        ts(A("PF%d" % (n % 4)), po, -2047.875, OP.add)
+
+    def xg(n):
+        gather_s(A("XG%d" % (n % 3)), A("X"), A("PO%d" % (n % 4)))
+
+    for q in range(8):
+        src, d = A("O", p0=16 * q, p1=16 * q + 16), A("OX", 128 * q, 128 * q + 128)
+        dma("dox", ap(d), ap(src), "Y", [src], [d])
+    og(0, 0); xg(0); og(1, 0); xg(1)
+    ts(A("DB"), A("IOT"), A("CF", 12, 13), OP.is_equal)
+    ts(A("WU"), A("I16"), A("CF", 8, 9), OP.is_equal, A("CF", 16, 17), OP.mult)
+    ts(A("DUB"), A("IOT"), A("CF", 12, 13), OP.is_equal, A("CF", 16, 17), OP.mult)
+    ts(A("HID"), A("ID"), 0.5, OP.mult); ts(A("NID"), A("ID"), -1.0, OP.mult)
+    ts(A("REP", p1=8), A("GF", p1=8), A("CF", 0, 1, p1=8), OP.is_equal)
+    ts(A("B8B"), A("I16"), A("CF", 8, 9), OP.is_equal)
+    cp(A("IOH"), A("IOT", 0, 128)); ts(A("IOB"), A("IOT", 0, 128), 1.0, OP.add)
+    ts(A("NREP", p1=8), A("REP", p1=8), -45.0, OP.mult)
+    ts(A("ZR", p1=1), A("O", 0, 512, p1=1), 0.0, OP.mult)
+
+    def round_(r):
+        last = r == RO - 1
+
+        def sub(n, b):
+            s, i = divmod(n, 3); d = "D%d" % ((4 * n + b) % 3); z = A("Z%d_%d" % (r, s), 128 * i, 128 * i + 128)
+            for j in range(4):
+                o = A(d, 128 * j, 128 * j + 128)
+                mm(o, A("FI"), A("XG%d" % (n % 3), 4 * b + j, 2048, 16), True, False); mm(o, A("NFI"), z, False, True)
+
+        def near(n, b):
+            ts(A("NR%d" % (n % 2), 512 * b, 512 * b + 512), A("D%d" % ((4 * n + b) % 3)), MAG, OP.add, MAG, OP.is_equal)
+
+        def tm(n, b):
+            if b == 0: mm(A("KEY", 0, 128), A("ONE", 0, 128, p1=1), A("KB", p1=1), True, False)
+            for k in range(4 * b, 4 * b + 4):
+                mm(A("KEY", k, 128, 16), A("NR%d" % (n % 2), 128 * k, 128 * k + 128), A("W8"), False, k == 15)
+
+        def pa(n):
+            s, i = divmod(n, 3); s1 = A("S1_%d" % s, 128 * i, 128 * i + 128); m = A("S1_%d" % s, 128 * i + 15, 128 * i + 128, 16)
+            run("V", [A("RST"), A("KEY", 0, 128)], [s1], lambda: g.vector.tensor_tensor_scan(ap(s1), ap(A("RST")), ap(A("KEY", 0, 128)), 0.0, OP.add, OP.max))
+            tick(2)
+            if s == 0: ts(A("MM"), m, THR0, OP.max)
+            else: tt(A("MM"), m, A("FL%d_%d" % (r, s), 16 * i + 8, 16 * i + 16), OP.max)
+            tick()
+            for q in range(8):
+                ts(A("NO%d" % (n % 2), 16 * q, 16 * q + 16), A("KEY", 16 * q, 16 * q + 16), A("MM", q, q + 1), OP.is_ge)
+            mm(A("MI", 0, 128), A("NO%d" % (n % 2)), A("ID"), True, True)
+
+        def pb(n):
+            s, i = divmod(n, 3); sl = "SEL%d" % (n % 2); m = A("S1_%d" % s, 128 * i + 15, 128 * i + 128, 16)
+            tt(A(sl), A("MI", 0, 128), A("PF%d" % (n % 4)), OP.mult)
+            for b in range(16):
+                mm(A("MI", 128, 136), A("DB", 15 - b, 143 - b), A(sl, b, 128, 16), b == 0, b == 15)
+            mm(A("MI", 136, 144), A(sl), A("B8"), True, True)
+            ts(A("QB%d" % s, 8 * i, 8 * i + 8), m, -7.5, OP.add, M16, OP.add)
+            go = A("GO%d_%d" % (r, s), 8 * i, 8 * i + 8)
+            if s == 0: ts(go, m, THR0, OP.is_gt)
+            else: tt(go, m, A("FL%d_%d" % (r, s), 16 * i + 8, 16 * i + 16), OP.is_gt)
+            if s < 2: ts(A("F%d_%d" % (r, s), 16 * i + 8, 16 * i + 16), A("QB%d" % s, 8 * i, 8 * i + 8), M16, OP.subtract, 15.5, OP.add)
+
+        def pc(n):
+            s, i = divmod(n, 3); L = A("MI", 128, 136)
+            ts(A("NF"), L, 0.0, OP.is_equal, 2048.0, OP.mult); tick()
+            t = A("F%d_%d" % (r, s), 16 * i, 16 * i + 8) if s < 2 else A("TF", 0, 8)
+            tt(t, L, A("NF"), OP.add); tick()
+            lu = A("LU%d_%d" % (r, s), 8 * i, 8 * i + 8)
+            ts(lu, t, 2048.0, OP.add)
+            if s < 2: send(nxt, A("FL%d_%d" % (r, s + 1), 16 * i, 16 * i + 16), A("F%d_%d" % (r, s), 16 * i, 16 * i + 16), "aF%d_%d_%d" % (r, s + 1, i))
+            act(A("UV%d" % r, 8 * i, 8 * i + 8) if s == 0 else A("VMB%d" % s, 8 * i, 8 * i + 8), A("MI", 136, 144), AF.Copy)
+            if s < 2:
+                zo = A("ZO%d_%d" % (r, s), 128 * i, 128 * i + 128)
+                gather_s(zo, A("X"), lu)
+                send(nxt, A("Z%d_%d" % (r, s + 1), 128 * i, 128 * i + 128), zo, "aZ%d_%d_%d" % (r, s + 1, i))
+            if i == 2:
+                if s == 0: send(nxt, A("UL%d" % r), A("UV%d" % r), "aU%d" % r)
+                else:
+                    send(prv, A("GL%d_%d" % (r, s)), A("GO%d_%d" % (r, s)), "aG%d_%d" % (r, s))
+                    send(T.cores[(rank - s) % N], A("LL%d_%d" % (r, s)), A("LU%d_%d" % (r, s)), "aL%d_%d" % (r, s))
+
+        def codes():
+            for i in range(3):
+                mm(A("MI", 256 + 8 * i, 264 + 8 * i), A("Z%d_0" % r, 128 * i, 128 * i + 128), A("WU"), True, True)
+            cp(A("IA"), A("MI", 256, 280)); ts(A("FA"), A("VL"), -2048.0, OP.add); ts(A("IB"), A("IA"), 4095, OP.bitwise_and)
+            for b in range(16):
+                mm(A("MI", 288, 312), A("DUB", 15 - b, 143 - b), A("Z%d_0" % r, b, 384, 16), b == 0, b == 15)
+            tt(A("IA"), A("MI", 288, 312), A("VL"), OP.add)
+            ts(A("FB"), A("IB"), 2048.0, OP.is_gt, -4096.0, OP.mult); ts(A("IC"), A("IA"), 4095, OP.bitwise_and)
+            tt(A("UV%d" % r, 24, 48), A("IB"), A("FB"), OP.add)
+            for i in range(3):
+                for a in range(8):
+                    ts(A("M0", 16 * a, 16 * a + 16), A("BM"), A("FA", 8 * i + a, 8 * i + a + 1), OP.mult)
+                mm(A("MI", 320 + 8 * i, 328 + 8 * i), A("M0"), A("B8"), True, True)
+            cp(A("VMB0"), A("MI", 320, 344))
+
+        def exdig(s):
+            v = A("VMB0") if s == 0 else A("UL%d" % r, 0, 24)
+
+            def xoh(j): return lambda: ts(A("XOH%d" % s, 128 * j, 128 * j + 128), A("IOH"), A("XC%d" % s, j, j + 1), OP.is_equal)
+            return [lambda: ts(A("EA"), v, 2048.0, OP.add), lambda: ts(A("EF"), A("QB%d" % s), M16, OP.subtract, 15.0, OP.add),
+                    lambda: ts(A("EB"), A("EA"), 127, OP.bitwise_and), lambda: tt(A("EG"), A("EF"), A("S1_%d" % s, 15, 384, 16), OP.subtract),
+                    lambda: cp(A("WL%d" % s), A("EB")), lambda: ts(A("EH"), A("EG"), 8.0, OP.mult),
+                    lambda: ts(A("EC"), A("EA"), 7, OP.arith_shift_right, 7, OP.bitwise_and),
+                    lambda: tt(A("XC%d" % s), A("EH"), A("EC"), OP.add)], [xoh(j) for j in range(24)]
+
+        def exmask(s):
+            def um():
+                tt(A("UM%d" % s), A("UV%d" % r, 24, 48) if s == 0 else A("UL%d" % r, 24, 48), A("GL%d_%d" % (r, s + 1)), OP.mult)
+                if s == 0:
+                    for h in range(2): mm(A("EX%d" % h), A("ZR", 0, 128, p1=1), A("ZR", p1=1), True, False)
+
+            def yu(j):
+                q = j % 8; y = A("YU", 128 * j, 128 * j + 128)
+                ts(y, A("IOH"), A("WL%d" % s, j, j + 1), OP.is_equal, A("UM%d" % s, j, j + 1), OP.mult)
+                mm(A("EX%d" % (q // 4), q % 4 * 128, q % 4 * 128 + 128), A("XOH%d" % s, 128 * j, 128 * j + 128), y, False, s == 1 and j in (19, 23))
+            return [um], [lambda j=j: yu(j) for j in range(24)]
+
+        def pendig(s, c0, c1):
+            v = A("UV%d" % r, c0, c1) if s == 0 else A("VMB%d" % s, c0, c1); a, b, c = A("PA", c0, c1), A("PB_", c0, c1), A("PC", c0, c1)
+
+            def lob():
+                ts(A("LOB%d" % s, c0, c1), b, -1.0, OP.mult, -0.5, OP.add)
+                for j in range(c0, c1):
+                    act(A("SG%d" % s, 34 * j, 34 * j + 33), A("IOT", 0, 33), AF.Sign, A("LOB%d" % s, j, j + 1))
+            return [lambda: ts(a, v, 2048.0, OP.add), lambda: ts(b, a, 31, OP.bitwise_and), lambda: ts(c, a, 5, OP.arith_shift_right),
+                    lob, lambda: ts(A("HP%d" % s, c0, c1), c, 1.0, OP.add)]
+
+        def penmask(s, c0, c1, first, end):
+            m = A("HM%d" % s, c0, c1); hp = A("HP%d" % s, c0, c1); go = A("GO%d_%d" % (r, s), c0, c1)
+
+            def hoh(j):
+                q = j % 8; h = A("HOH", 128 * j, 128 * j + 128)
+                if first and j == c0: mm(A("PEN", 0, 264), A("ZR", 0, 128, p1=1), A("ZR", 0, 264, p1=1), True, False)
+                ts(h, A("IOB"), A("HM%d" % s, j, j + 1), OP.is_equal)
+                mm(A("PEN", 33 * q, 33 * q + 33), h, A("SG%d" % s, 34 * j, 34 * j + 33), False, end and j == 23)
+            if s < 2: pre = [lambda: tt(A("FC%d" % s, c0, c1), go, A("GL%d_%d" % (r, s + 1), c0, c1), OP.subtract), lambda: tt(m, hp, A("FC%d" % s, c0, c1), OP.mult)]
+            else: pre = [lambda: tt(m, hp, go, OP.mult)]
+            return pre, [lambda j=j: hoh(j) for j in range(c0, c1)]
+
+        def settle():
+            def alive(s, i): return lambda: ts(A("AL", 24 * s - 24 + 8 * i, 24 * s - 16 + 8 * i), A("FL%d_%d" % (r, s), 16 * i, 16 * i + 8), 2047.75, OP.is_le)
+
+            def m1():
+                cp(A("AC"), A("AR"))
+                for i in range(3): mm(A("MI", 352, 353, p1=8), A("QT", 8 * i, 8 * i + 8), A("ONE", 0, 1), i == 0, False)
+                mm(A("MI", 352, 353, p1=8), A("B8B"), A("AC"), False, True)
+                cp(A("AI", p1=8), A("MI", 352, 353, p1=8))
+
+            def m2():
+                cp(A("AB", p1=8), A("AJ", p1=8))
+                mm(A("MI", 360, 361), A("REP", p1=8), A("AB", p1=8), True, True)
+                ts(A("FCOL"), A("MI", 360, 361), -0.0625 / 64, OP.mult, 1.5625 / 64, OP.add)
+            return [lambda: ts(A("QA"), A("GO%d_0" % r), -1.0, OP.mult, 1.0, OP.add)] + [alive(s, i) for s in (1, 2) for i in range(3)] + [
+                lambda: tt(A("QT"), A("QA"), A("GO%d_1" % r), OP.subtract),
+                lambda: run("V", [A("AL")], [A("AR")], lambda: g.vector.tensor_reduce(ap(A("AR")), ap(A("AL")), AxisListType.X, OP.add)),
+                m1, lambda: ts(A("AJ", p1=8), A("AI", p1=8), 3, OP.bitwise_and), m2]
+
+        def boats():
+            o = [lambda: cp(A("FA"), A("IC"))]
+            for lu in (A("LU%d_0" % r), A("LL%d_1" % r), A("LL%d_2" % r)):
+                o += [lambda lu=lu: cp(A("BA"), lu), lambda lu=lu: ts(A("BB"), lu, 4096.0, OP.is_ge), lambda: tt(A("BC"), A("FA"), A("BA"), OP.subtract),
+                      lambda: tt(A("BD"), A("BC"), A("BB"), OP.mult), lambda: tt(A("FA"), A("BD"), A("BA"), OP.add)]
+            if last: return o + [lambda: dma("oyv", T.yv[:, :], ap(A("FA")), "Y", [A("FA")], [])]
+            return o + [lambda: cp(A("VL"), A("FA")), lambda: ts(A("LWI"), A("VL"), 1023, OP.bitwise_and), lambda: cp(A("LW"), A("LWI"))]
+
+        z0, z1, zn, y = A("Z%d_0" % r), A("ZO%d_0" % r), A("Z%d_0" % (r + 1)) if not last else A("RD"), A("PEN", 0, 384)
+
+        def own(part):
+            if part == 0:
+                mm(y, A("HID"), z0, True, False); mm(y, A("HID"), z1, False, False); mm(y, A("QROW", p1=1), A("ONE", p1=1), False, True)
+                ts(A("RN"), z1, 256.0, OP.is_ge)
+                act(A("RY"), y, AF.Copy, MAG); act(A("RB"), A("RY"), AF.Copy, -MAG)
+            if part == 1:
+                mm(y, A("ID"), z0, True, False); mm(y, A("NID"), A("RB"), False, True)
+                tt(A("RE"), y, A("RN"), OP.mult)
+            if part == 2:
+                mm(y, A("ID"), A("RE"), True, False); mm(y, A("ID"), A("RB"), False, True)
+                act(zn, y, AF.Copy)
+                if last: dma("oyv", T.yz[:, :], ap(zn), "Y", [zn], [])
+
+        if r: og(1, r); xg(1)
+        codes()
+        for n in range(9):
+            s, i = divmod(n, 3)
+            if i == 0 and n:
+                pa(n - 1); tick(4); pb(n - 1); tick(5); pc(n - 1)
+                og(n + 1, r); xg(n + 1)
+                e, x = exdig(s - 1)
+                fq.extend(weave(e, pendig(s - 1, 0, 24)) + (weave(x, settle()) if s == 2 and not last else x))
+            sub(n, 0); sub(n, 1); sub(n, 2)
+            if i == 0 and n: tick(20)
+            if n == 7:
+                e, x = penmask(0, 0, 24, True, False); e2, x2 = exmask(0)
+                fq.extend(e[:1] + e2 + e[1:] + x + x2)
+            for b in range(4):
+                near(n, b)
+                if b == 0:
+                    if i: pa(n - 1)
+                    sub(n, 3)
+                if b == 1 and i: pb(n - 1)
+                if b == 2:
+                    if i: tick(2); pc(n - 1)
+                    if i == 0: og(n + 2, r); xg(n + 2)
+                    if i == 2 and n < 8: og(n + 1, r); xg(n + 1)
+                tm(n, b); tick(3)
+            if n in (3, 5, 6): own((3, 5, 6).index(n))
+        e, x = penmask(2, 0, 16, False, False)
+        fq.extend(pendig(2, 0, 16) + e + x)
+        pa(8); tick(4); pb(8); tick(6); pc(8)
+        if not last: fq.extend([lambda: ts(A("FI"), A("ID"), A("FCOL"), OP.mult), lambda: ts(A("NFI"), A("ID"), A("FCOL"), OP.mult, -1.0, OP.mult)])
+        d = pendig(2, 16, 24); e, x = penmask(2, 16, 24, False, False); e1, x1 = penmask(1, 0, 24, False, True); e2, x2 = exmask(1)
+        tick(4); fq.extend(d); tick(10); fq.extend(e + x + e1[:1] + e2 + e1[1:] + x1); tick(999)
+        act(A("HC0"), A("PEN", 0, 264), AF.Copy)
+        fq.extend(x2); tick(8)
+        tt(A("HC", 0, 263), A("HC0", 1, 264), A("HC0", 0, 263), OP.is_gt)
+        for q in range(8):
+            src, d = A("HC", 33 * q, 33 * q + 32), A("HS", p0=q, p1=q + 1)
+            dma("dhs", ap(d), ap(src), "Y", [src], [d])
+        tick(999)
+        fq.extend(boats())
+        for h in range(2):
+            c = (512 * h, 512 * h + 512)
+            tick(2); tt(A("OT", *c), A("EX%d" % h), A("OX", *c), OP.add); tick(1); ts(A("OX", *c), A("OT", *c), 4095, OP.bitwise_and)
+            for q in range(4 * h, 4 * h + 4):
+                src, d = A("OX", 128 * q, 128 * q + 128), A("O", p0=16 * q, p1=16 * q + 16)
+                dma("dex", ap(d), ap(src), "Y", [src], [d])
+        tick(999)
+        for c in range(8):
+            d = A("D%d" % (c % 3)); x = A("X", 512 * c, 512 * c + 512)
+            mm(d, A("ID"), x, True, False); mm(d, A("NREP", p1=8), A("HS", 512 * c, 512 * c + 512, p1=8), False, True)
+            if c % 2: ts(x, d, 0.0, OP.max)
+            else: act(x, d, AF.Relu)
+            if last: dma("oyx%d" % (c % 2), T.yx[:, 512 * c:512 * c + 512], ap(x), "Y", [x], [])
+        if last:
+            ts(A("EXS"), A("O", 512, 1024), 4096.0, OP.mult); tt(A("YN"), A("EXS"), A("O", 0, 512), OP.add)
+            dma("oyn", T.yn[:, :], ap(A("YN")), "Y", [A("YN")], [])
+        else: og(0, r + 1); xg(0)
+
+    for r in range(RO):
+        round_(r)
+    for sem in cnt:
+        if known["G"].get(sem, 0) < cnt[sem]: g.wait_ge(T.sem[sem], cnt[sem])

@@ -16,20 +16,20 @@ def _s(names, cols, dtype):
         ALIAS[n] = ("pool_" + dtype, o, cols); POOL[dtype] = o + (cols + w - 1) // w * w
 
 
-_b("X", 4112, "bfloat16"); _b("O OX OT", 1024, "int32"); _b("NB", 512, "int32"); _b("YN EXS", 512, "float32")
+_b("X", 4112, "bfloat16"); _b("O", 4112, "int32"); _b("OX OT OE", 1024, "int32"); _b("NB", 512, "int32"); _b("YN EXS", 512, "float32")
 _b("XG0 XG1 XG2 NR0 NR1", 2048, "bfloat16"); _b("PO0 PO1 PO2 PO3", 128, "uint16"); _b("PF0 PF1 PF2 PF3 SEL0 SEL1 M0 IOH", 128, "float16")
 _b("D0 D1 D2 KEY MI EX0 EX1 PEN", 512, "float32", "psum"); _b("NO0 NO1", 128, "bfloat16")
 _b("S1_0 S1_1 S1_2", 384, "float32"); _b("SG0 SG1 SG2", 24 * 34, "bfloat16"); _b("XOH0 XOH1 YU", 24 * 128, "float16"); _b("HOH", 24 * 128, "bfloat16")
-_s("VMB0 VMB1 VMB2 QB0 QB1 QB2 LOB0 LOB1 LOB2 HP0 HP1 HP2 XC0 XC1 WL0 WL1 FA FB FC BA BB BC BD EF EG EH TF HM0 HM1 HM2 FC0 FC1 UM0 UM1 CF", 24, "float32")
-_s("VL IA IB IC LWI OA OB EA EB EC PA PB_ PC", 24, "int32"); _s("LW", 24, "uint16"); _s("NF MM PB I16", 8, "float32"); _s("QA QT", 24, "bfloat16")
+_s("VMB0 VMB1 VMB2 QB0 QB1 QB2 LOB0 LOB1 LOB2 HP0 HP1 HP2 XC0 XC1 WL0 WL1 FA FB FC BB BC BD EF EG EH HM0 HM1 HM2 FC0 FC1 UM0 UM1 CF", 24, "float32")
+_s("VL IA IB IC LWI BI EA EB EC PA PB_ PC", 24, "int32"); _s("LW", 24, "uint16"); _s("MM PB I16", 8, "float32"); _s("QA QT", 24, "bfloat16")
 for _r in range(RO):
     for _i in range(3):
         _b("Z%d_%d" % (_r, _i), 384, "bfloat16")
         _s("GO%d_%d" % (_r, _i), 24, "float32"); _s("LU%d_%d" % (_r, _i), 24, "uint16")
         if _i < 2:
-            _s("F%d_%d" % (_r, _i), 48, "float32"); _b("ZO%d_%d" % (_r, _i), 384, "bfloat16")
+            _s("F%d_%d" % (_r, _i), 24, "float32"); _b("ZO%d_%d" % (_r, _i), 384, "bfloat16")
         if _i > 0:
-            _s("FL%d_%d" % (_r, _i), 48, "float32"); _s("GL%d_%d" % (_r, _i), 24, "float32"); _s("LL%d_%d" % (_r, _i), 24, "uint16")
+            _s("FL%d_%d GL%d_%d" % (_r, _i, _r, _i), 24, "float32"); _s("LV%d_%d LL%d_%d" % (_r, _i, _r, _i), 24, "uint16")
     _s("UV%d UL%d" % (_r, _r), 48, "float32")
 _b("HC0", 264, "float32"); _b("HC", 264, "bfloat16"); _b("HS", 4096, "bfloat16")
 _b("RY", 384, "float32"); _b("RB RN RE RD ONE", 384, "bfloat16")
@@ -40,16 +40,17 @@ _s("AL", 48, "float32"); _s("AR FCOL", 1, "float32"); _s("AC AB", 1, "bfloat16")
 for _d in POOL:
     _b("pool_" + _d, POOL[_d], _d)
 
-SEMAPHORES = ["V", "S", "P", "G", "ls", "dnb", "dv", "dz", "dx0", "dx1", "dx2", "dx3", "dhs", "dex", "dox", "oyx0", "oyx1", "oyn", "oyv"]
+SEMAPHORES = ["V", "S", "P", "G", "ls", "dnb", "dv", "dz", "dx0", "dx1", "dx2", "dx3", "dhs", "dex", "dox", "dcp", "oyx0", "oyx1", "oyn", "oyv"]
 for _r in range(RO):
     for _j in (1, 2):
         for _i in range(NCH):
-            SEMAPHORES += ["aF%d_%d_%d" % (_r, _j, _i), "aZ%d_%d_%d" % (_r, _j, _i)]
+            SEMAPHORES += ["aF%d_%d_%d" % (_r, _j, _i), "aV%d_%d_%d" % (_r, _j, _i), "aZ%d_%d_%d" % (_r, _j, _i)]
         SEMAPHORES += ["aG%d_%d" % (_r, _j), "aL%d_%d" % (_r, _j)]
     SEMAPHORES += ["aU%d" % _r]
 
 MAG = 12582912.0
 M16 = 201326592.0
+UP, DOWN, EPS = 4097 / 4096, 4095 / 4096, 0.00015
 THR0 = 16.0 * (34816 + 1) - 0.5
 
 
@@ -75,7 +76,7 @@ def rank_program(g, core, T, topo):
     def span(a):
         w = BS[SCRATCH[a[0]][2]]
         if SCRATCH[a[0]][0] == "psum": return (0, 128, 0, 2048)
-        return (a[4], a[5], a[1] * w // 16 * 16, (a[2] * w + 15) // 16 * 16)
+        return (a[4], a[5], a[1] * w, a[2] * w)
 
     def learn(q, comp, n):
         k = known[q]
@@ -90,7 +91,8 @@ def rank_program(g, core, T, topo):
             for a in lst:
                 ps = SCRATCH[a[0]][0] == "psum"; s = span(a)
                 for (t, ow, oc, on, oq) in acc.get(a[0], []):
-                    if not (s[0] < t[1] and t[0] < s[1] and s[2] < t[3] and t[2] < s[3]): continue
+                    b = 16 if ow and w and (oc in eng) != (comp in eng) else 1
+                    if not (s[0] < t[1] and t[0] < s[1] and s[2] // b * b < -(-t[3] // b) * b and t[2] // b * b < -(-s[3] // b) * b): continue
                     if ps:
                         if oq == q and oc == comp and (q == "P" or not (ow or w)): continue
                     elif not (ow or w): continue
@@ -181,16 +183,18 @@ def rank_program(g, core, T, topo):
     for r in range(RO):
         for s in (1, 2):
             for i in range(NCH):
-                arrives("aF%d_%d_%d" % (r, s, i), A("FL%d_%d" % (r, s), 16 * i, 16 * i + 16), prv)
+                arrives("aF%d_%d_%d" % (r, s, i), A("FL%d_%d" % (r, s), 8 * i, 8 * i + 8), prv)
+                arrives("aV%d_%d_%d" % (r, s, i), A("LV%d_%d" % (r, s), 8 * i, 8 * i + 8), prv)
                 arrives("aZ%d_%d_%d" % (r, s, i), A("Z%d_%d" % (r, s), 128 * i, 128 * i + 128), prv)
             arrives("aG%d_%d" % (r, s), A("GL%d_%d" % (r, s)), nxt)
             arrives("aL%d_%d" % (r, s), A("LL%d_%d" % (r, s)), T.cores[(rank + s) % N])
         arrives("aU%d" % r, A("UL%d" % r), prv)
 
+    ms(A("X", 2048, 2049), 512.0); ms(A("O", 2048, 2049), 0)
     dma("dnb", ap(A("NB")), T.nb[:, :], "Y", [], [A("NB")])
     dma("dv", ap(A("VL")), T.v[:, :], "S", [], [A("VL")])
     for i in range(4):
-        a = A("X", 1024 * i, 1024 * i + 1024)
+        a = A("X", 1024 * i + i // 2, 1024 * i + i // 2 + 1024)
         dma("dx%d" % i, ap(a), T.tracks[:, 1024 * i:1024 * i + 1024], "YS"[i % 2], [], [a])
     dma("dz", ap(A("Z0_0")), T.z[:, :], "Y", [], [A("Z0_0")])
     iota(A("CI", 0, 1), [[1, 1]], 0, 1, False)
@@ -199,7 +203,8 @@ def rank_program(g, core, T, topo):
     iota(A("KB", p1=1), [[0, 8], [-1, 16]], 15, 0)
     iota(A("KF"), [[0, 8], [1, 16]], 0, 0)
     iota(A("GF"), [[1, 8], [0, 16]], 0, 0)
-    ms(A("X", 4096, 4112), 512.0); ms(A("ONE"), 1.0); ms(A("QROW", p1=1), -0.25); ms(A("PB", 4, 5), 524288.0)
+    ms(A("X", 4097, 4112), 512.0); ms(A("O", 4097, 4112), 0)
+    ms(A("ONE"), 1.0); ms(A("QROW", p1=1), -0.25); ms(A("PB", 4, 5), 524288.0)
     cp(A("CF", 0, 1), A("CI", 0, 1))
     ts(A("CI", 4, 5), A("CI", 0, 1), 15, OP.bitwise_and); cp(A("CF", 4, 5), A("CI", 4, 5))
     ts(A("ID"), A("IOT", 0, 128), A("CF", 0, 1), OP.is_equal)
@@ -217,25 +222,27 @@ def rank_program(g, core, T, topo):
     ts(A("B8"), A("I16"), A("CF", 8, 9), OP.is_equal)
     cp(A("LW"), A("LWI"))
     ts(A("BM"), A("IOT", 0, 16), A("CF", 4, 5), OP.is_equal)
-    ts(A("O", 0, 512), A("NB"), 4095, OP.bitwise_and)
-    ts(A("O", 512, 1024), A("NB"), 12, OP.arith_shift_right)
+    ts(A("OT", 0, 512), A("NB"), 4095, OP.bitwise_and); ts(A("OT", 512, 1024), A("NB"), 12, OP.arith_shift_right)
+    ts(A("O", 0, 512), A("OT", 0, 512), UP, OP.mult, EPS, OP.add); ts(A("O", 512, 1024), A("OT", 512, 1024), UP, OP.mult, EPS, OP.add)
 
     def og(n, r):
         s, i = divmod(n, 3)
-        if s:
-            f = A("FL%d_%d" % (r, s), 16 * i, 16 * i + 8); c = (8 * i, 8 * i + 8)
-            ts(A("OA", *c), f, 2048.0, OP.add); tick(); ts(A("OB", *c), A("OA", *c), 1023, OP.bitwise_and); tick(); cp(A("LW", *c), A("OB", *c)); tick()
-        po = A("PO%d" % (n % 4))
-        gather_v(po, A("O"), A("LW", 8 * i, 8 * i + 8)); tick()
-        ts(A("PF%d" % (n % 4)), po, -2047.875, OP.add)
+        po = A("PO%d" % (n % 4)); l = A("LV%d_%d" % (r, s), 8 * i, 8 * i + 8) if s else A("LW", 8 * i, 8 * i + 8)
+        gather_v(po, A("O", 0, 4112) if s else A("O", 0, 1024), l); tick()
+        ts(A("PF%d" % (n % 4)), po, -2048.0, OP.add)
+
+    def copies():
+        for a in (1024, 2049, 3073):
+            src, d = A("O", 0, 1024), A("O", a, a + 1024)
+            dma("dcp", ap(d), ap(src), "Y", [src], [d])
 
     def xg(n):
         gather_s(A("XG%d" % (n % 3)), A("X"), A("PO%d" % (n % 4)))
 
     for q in range(8):
-        src, d = A("O", p0=16 * q, p1=16 * q + 16), A("OX", 128 * q, 128 * q + 128)
+        src, d = A("OT", p0=16 * q, p1=16 * q + 16), A("OX", 128 * q, 128 * q + 128)
         dma("dox", ap(d), ap(src), "Y", [src], [d])
-    og(0, 0); xg(0); og(1, 0); xg(1)
+    og(0, 0); xg(0); og(1, 0); xg(1); copies()
     ts(A("DB"), A("IOT"), A("CF", 12, 13), OP.is_equal)
     ts(A("WU"), A("I16"), A("CF", 8, 9), OP.is_equal, A("CF", 16, 17), OP.mult)
     ts(A("DUB"), A("IOT"), A("CF", 12, 13), OP.is_equal, A("CF", 16, 17), OP.mult)
@@ -255,24 +262,24 @@ def rank_program(g, core, T, topo):
                 o = A(d, 128 * j, 128 * j + 128)
                 mm(o, A("FI"), A("XG%d" % (n % 3), 4 * b + j, 2048, 16), True, False); mm(o, A("NFI"), z, False, True)
 
-        def near(n, b):
-            ts(A("NR%d" % (n % 2), 512 * b, 512 * b + 512), A("D%d" % ((4 * n + b) % 3)), MAG, OP.add, MAG, OP.is_equal)
+        def near(n, b, h):
+            ts(A("NR%d" % (n % 2), 512 * b + 256 * h, 512 * b + 256 * h + 256), A("D%d" % ((4 * n + b) % 3), 256 * h, 256 * h + 256), MAG, OP.add, MAG, OP.is_equal)
 
         def tm(n, b):
             if b == 0: mm(A("KEY", 0, 128), A("ONE", 0, 128, p1=1), A("KB", p1=1), True, False)
             for k in range(4 * b, 4 * b + 4):
                 mm(A("KEY", k, 128, 16), A("NR%d" % (n % 2), 128 * k, 128 * k + 128), A("W8"), False, k == 15)
 
-        def pa(n):
+        def pa(n, step):
             s, i = divmod(n, 3); s1 = A("S1_%d" % s, 128 * i, 128 * i + 128); m = A("S1_%d" % s, 128 * i + 15, 128 * i + 128, 16)
-            run("V", [A("RST"), A("KEY", 0, 128)], [s1], lambda: g.vector.tensor_tensor_scan(ap(s1), ap(A("RST")), ap(A("KEY", 0, 128)), 0.0, OP.add, OP.max))
-            tick(2)
-            if s == 0: ts(A("MM"), m, THR0, OP.max)
-            else: tt(A("MM"), m, A("FL%d_%d" % (r, s), 16 * i + 8, 16 * i + 16), OP.max)
-            tick()
-            for q in range(8):
-                ts(A("NO%d" % (n % 2), 16 * q, 16 * q + 16), A("KEY", 16 * q, 16 * q + 16), A("MM", q, q + 1), OP.is_ge)
-            mm(A("MI", 0, 128), A("NO%d" % (n % 2)), A("ID"), True, True)
+            if step == 0: run("V", [A("RST"), A("KEY", 0, 128)], [s1], lambda: g.vector.tensor_tensor_scan(ap(s1), ap(A("RST")), ap(A("KEY", 0, 128)), 0.0, OP.add, OP.max))
+            elif step == 1:
+                if s == 0: ts(A("MM"), m, THR0, OP.max)
+                else: tt(A("MM"), m, A("FL%d_%d" % (r, s), 8 * i, 8 * i + 8), OP.max)
+            else:
+                for q in range(8):
+                    ts(A("NO%d" % (n % 2), 16 * q, 16 * q + 16), A("KEY", 16 * q, 16 * q + 16), A("MM", q, q + 1), OP.is_ge)
+                mm(A("MI", 0, 128), A("NO%d" % (n % 2)), A("ID"), True, True)
 
         def pb(n):
             s, i = divmod(n, 3); sl = "SEL%d" % (n % 2); m = A("S1_%d" % s, 128 * i + 15, 128 * i + 128, 16)
@@ -283,19 +290,17 @@ def rank_program(g, core, T, topo):
             ts(A("QB%d" % s, 8 * i, 8 * i + 8), m, -7.5, OP.add, M16, OP.add)
             go = A("GO%d_%d" % (r, s), 8 * i, 8 * i + 8)
             if s == 0: ts(go, m, THR0, OP.is_gt)
-            else: tt(go, m, A("FL%d_%d" % (r, s), 16 * i + 8, 16 * i + 16), OP.is_gt)
-            if s < 2: ts(A("F%d_%d" % (r, s), 16 * i + 8, 16 * i + 16), A("QB%d" % s, 8 * i, 8 * i + 8), M16, OP.subtract, 15.5, OP.add)
+            else: tt(go, m, A("FL%d_%d" % (r, s), 8 * i, 8 * i + 8), OP.is_gt)
+            if s < 2: ts(A("F%d_%d" % (r, s), 8 * i, 8 * i + 8), A("QB%d" % s, 8 * i, 8 * i + 8), M16, OP.subtract, 15.5, OP.add)
 
         def pc(n):
-            s, i = divmod(n, 3); L = A("MI", 128, 136)
-            ts(A("NF"), L, 0.0, OP.is_equal, 2048.0, OP.mult); tick()
-            t = A("F%d_%d" % (r, s), 16 * i, 16 * i + 8) if s < 2 else A("TF", 0, 8)
-            tt(t, L, A("NF"), OP.add); tick()
-            lu = A("LU%d_%d" % (r, s), 8 * i, 8 * i + 8)
-            ts(lu, t, 2048.0, OP.add)
-            if s < 2: send(nxt, A("FL%d_%d" % (r, s + 1), 16 * i, 16 * i + 16), A("F%d_%d" % (r, s), 16 * i, 16 * i + 16), "aF%d_%d_%d" % (r, s + 1, i))
-            act(A("UV%d" % r, 8 * i, 8 * i + 8) if s == 0 else A("VMB%d" % s, 8 * i, 8 * i + 8), A("MI", 136, 144), AF.Copy)
+            s, i = divmod(n, 3); c = (8 * i, 8 * i + 8)
+            lu = A("LU%d_%d" % (r, s), *c)
+            ts(lu, A("MI", 128, 136), 2048.0, OP.add)
+            if s < 2: send(nxt, A("LV%d_%d" % (r, s + 1), *c), lu, "aV%d_%d_%d" % (r, s + 1, i))
+            act(A("UV%d" % r, *c) if s == 0 else A("VMB%d" % s, *c), A("MI", 136, 144), AF.Copy)
             if s < 2:
+                send(nxt, A("FL%d_%d" % (r, s + 1), *c), A("F%d_%d" % (r, s), *c), "aF%d_%d_%d" % (r, s + 1, i))
                 zo = A("ZO%d_%d" % (r, s), 128 * i, 128 * i + 128)
                 gather_s(zo, A("X"), lu)
                 send(nxt, A("Z%d_%d" % (r, s + 1), 128 * i, 128 * i + 128), zo, "aZ%d_%d_%d" % (r, s + 1, i))
@@ -324,7 +329,7 @@ def rank_program(g, core, T, topo):
             v = A("VMB0") if s == 0 else A("UL%d" % r, 0, 24)
 
             def xoh(j): return lambda: ts(A("XOH%d" % s, 128 * j, 128 * j + 128), A("IOH"), A("XC%d" % s, j, j + 1), OP.is_equal)
-            return [lambda: ts(A("EA"), v, 2048.0, OP.add), lambda: ts(A("EF"), A("QB%d" % s), M16, OP.subtract, 15.0, OP.add),
+            return [lambda: ts(A("EA"), v, 2048.0, OP.add, DOWN if s else 1.0, OP.mult), lambda: ts(A("EF"), A("QB%d" % s), M16, OP.subtract, 15.0, OP.add),
                     lambda: ts(A("EB"), A("EA"), 127, OP.bitwise_and), lambda: tt(A("EG"), A("EF"), A("S1_%d" % s, 15, 384, 16), OP.subtract),
                     lambda: cp(A("WL%d" % s), A("EB")), lambda: ts(A("EH"), A("EG"), 8.0, OP.mult),
                     lambda: ts(A("EC"), A("EA"), 7, OP.arith_shift_right, 7, OP.bitwise_and),
@@ -349,7 +354,7 @@ def rank_program(g, core, T, topo):
                 ts(A("LOB%d" % s, c0, c1), b, -1.0, OP.mult, -0.5, OP.add)
                 for j in range(c0, c1):
                     act(A("SG%d" % s, 34 * j, 34 * j + 33), A("IOT", 0, 33), AF.Sign, A("LOB%d" % s, j, j + 1))
-            return [lambda: ts(a, v, 2048.0, OP.add), lambda: ts(b, a, 31, OP.bitwise_and), lambda: ts(c, a, 5, OP.arith_shift_right),
+            return [lambda: ts(a, v, 2048.0, OP.add, DOWN, OP.mult), lambda: ts(b, a, 31, OP.bitwise_and), lambda: ts(c, a, 5, OP.arith_shift_right),
                     lob, lambda: ts(A("HP%d" % s, c0, c1), c, 1.0, OP.add)]
 
         def penmask(s, c0, c1, first, end):
@@ -365,7 +370,7 @@ def rank_program(g, core, T, topo):
             return pre, [lambda j=j: hoh(j) for j in range(c0, c1)]
 
         def settle():
-            def alive(s, i): return lambda: ts(A("AL", 24 * s - 24 + 8 * i, 24 * s - 16 + 8 * i), A("FL%d_%d" % (r, s), 16 * i, 16 * i + 8), 2047.75, OP.is_le)
+            def alive(s): return lambda: ts(A("AL", 24 * s - 24, 24 * s), A("LV%d_%d" % (r, s)), 2048.0, OP.not_equal)
 
             def m1():
                 cp(A("AC"), A("AR"))
@@ -377,7 +382,7 @@ def rank_program(g, core, T, topo):
                 cp(A("AB", p1=8), A("AJ", p1=8))
                 mm(A("MI", 360, 361), A("REP", p1=8), A("AB", p1=8), True, True)
                 ts(A("FCOL"), A("MI", 360, 361), -0.0625 / 64, OP.mult, 1.5625 / 64, OP.add)
-            return [lambda: ts(A("QA"), A("GO%d_0" % r), -1.0, OP.mult, 1.0, OP.add)] + [alive(s, i) for s in (1, 2) for i in range(3)] + [
+            return [lambda: ts(A("QA"), A("GO%d_0" % r), -1.0, OP.mult, 1.0, OP.add), alive(1), alive(2),
                 lambda: tt(A("QT"), A("QA"), A("GO%d_1" % r), OP.subtract),
                 lambda: run("V", [A("AL")], [A("AR")], lambda: g.vector.tensor_reduce(ap(A("AR")), ap(A("AL")), AxisListType.X, OP.add)),
                 m1, lambda: ts(A("AJ", p1=8), A("AI", p1=8), 3, OP.bitwise_and), m2]
@@ -385,8 +390,8 @@ def rank_program(g, core, T, topo):
         def boats():
             o = [lambda: cp(A("FA"), A("IC"))]
             for lu in (A("LU%d_0" % r), A("LL%d_1" % r), A("LL%d_2" % r)):
-                o += [lambda lu=lu: cp(A("BA"), lu), lambda lu=lu: ts(A("BB"), lu, 4096.0, OP.is_ge), lambda: tt(A("BC"), A("FA"), A("BA"), OP.subtract),
-                      lambda: tt(A("BD"), A("BC"), A("BB"), OP.mult), lambda: tt(A("FA"), A("BD"), A("BA"), OP.add)]
+                o += [lambda lu=lu: ts(A("BI"), lu, DOWN, OP.mult), lambda lu=lu: ts(A("BB"), lu, 2048.0, OP.is_equal), lambda: tt(A("BC"), A("FA"), A("BI"), OP.subtract),
+                      lambda: tt(A("BD"), A("BC"), A("BB"), OP.mult), lambda: tt(A("FA"), A("BD"), A("BI"), OP.add)]
             if last: return o + [lambda: dma("oyv", T.yv[:, :], ap(A("FA")), "Y", [A("FA")], [])]
             return o + [lambda: cp(A("VL"), A("FA")), lambda: ts(A("LWI"), A("VL"), 1023, OP.bitwise_and), lambda: cp(A("LW"), A("LWI"))]
 
@@ -410,30 +415,34 @@ def rank_program(g, core, T, topo):
         for n in range(9):
             s, i = divmod(n, 3)
             if i == 0 and n:
-                pa(n - 1); tick(4); pb(n - 1); tick(5); pc(n - 1)
+                pa(n - 1, 0); tick(2); pa(n - 1, 1); tick(2); pa(n - 1, 2); tick(4); pb(n - 1); tick(8); pc(n - 1)
                 og(n + 1, r); xg(n + 1)
                 e, x = exdig(s - 1)
                 fq.extend(weave(e, pendig(s - 1, 0, 24)) + (weave(x, settle()) if s == 2 and not last else x))
             sub(n, 0); sub(n, 1); sub(n, 2)
-            if i == 0 and n: tick(20)
+            if i == 0 and n: tick(8)
             if n == 7:
                 e, x = penmask(0, 0, 24, True, False); e2, x2 = exmask(0)
                 fq.extend(e[:1] + e2 + e[1:] + x + x2)
             for b in range(4):
-                near(n, b)
-                if b == 0:
-                    if i: pa(n - 1)
-                    sub(n, 3)
-                if b == 1 and i: pb(n - 1)
+                near(n, b, 0)
+                if i and b == 0: pa(n - 1, 0)
+                if i and b == 1: pa(n - 1, 2)
+                near(n, b, 1)
+                if b == 0: sub(n, 3)
+                if i and b == 0: pa(n - 1, 1)
+                if b == 1: tm(n, 0)
+                if i and b == 1: tick(2); pb(n - 1)
+                if i and b == 2: pc(n - 1)
+                if b: tm(n, b)
                 if b == 2:
-                    if i: tick(2); pc(n - 1)
                     if i == 0: og(n + 2, r); xg(n + 2)
                     if i == 2 and n < 8: og(n + 1, r); xg(n + 1)
-                tm(n, b); tick(3)
+                tick(2)
             if n in (3, 5, 6): own((3, 5, 6).index(n))
         e, x = penmask(2, 0, 16, False, False)
         fq.extend(pendig(2, 0, 16) + e + x)
-        pa(8); tick(4); pb(8); tick(6); pc(8)
+        pa(8, 0); tick(2); pa(8, 1); tick(2); pa(8, 2); tick(5); pb(8); tick(8); pc(8)
         if not last: fq.extend([lambda: ts(A("FI"), A("ID"), A("FCOL"), OP.mult), lambda: ts(A("NFI"), A("ID"), A("FCOL"), OP.mult, -1.0, OP.mult)])
         d = pendig(2, 16, 24); e, x = penmask(2, 16, 24, False, False); e1, x1 = penmask(1, 0, 24, False, True); e2, x2 = exmask(1)
         tick(4); fq.extend(d); tick(10); fq.extend(e + x + e1[:1] + e2 + e1[1:] + x1); tick(999)
@@ -448,12 +457,13 @@ def rank_program(g, core, T, topo):
         for h in range(2):
             c = (512 * h, 512 * h + 512)
             tick(2); tt(A("OT", *c), A("EX%d" % h), A("OX", *c), OP.add); tick(1); ts(A("OX", *c), A("OT", *c), 4095, OP.bitwise_and)
+            if not last: tick(1); ts(A("OE", *c), A("OX", *c), UP, OP.mult, EPS, OP.add)
             for q in range(4 * h, 4 * h + 4):
-                src, d = A("OX", 128 * q, 128 * q + 128), A("O", p0=16 * q, p1=16 * q + 16)
+                src, d = A("OX" if last else "OE", 128 * q, 128 * q + 128), A("O", 0, 1024, p0=16 * q, p1=16 * q + 16)
                 dma("dex", ap(d), ap(src), "Y", [src], [d])
         tick(999)
         for c in range(8):
-            d = A("D%d" % (c % 3)); x = A("X", 512 * c, 512 * c + 512)
+            d = A("D%d" % (c % 3)); x = A("X", 512 * c + c // 4, 512 * c + c // 4 + 512)
             mm(d, A("ID"), x, True, False); mm(d, A("NREP", p1=8), A("HS", 512 * c, 512 * c + 512, p1=8), False, True)
             if c % 2: ts(x, d, 0.0, OP.max)
             else: act(x, d, AF.Relu)
@@ -461,7 +471,7 @@ def rank_program(g, core, T, topo):
         if last:
             ts(A("EXS"), A("O", 512, 1024), 4096.0, OP.mult); tt(A("YN"), A("EXS"), A("O", 0, 512), OP.add)
             dma("oyn", T.yn[:, :], ap(A("YN")), "Y", [A("YN")], [])
-        else: og(0, r + 1); xg(0)
+        else: og(0, r + 1); xg(0); copies()
 
     for r in range(RO):
         round_(r)

@@ -1,6 +1,7 @@
 from concourse.mybir import dt, AluOpType as OP, ActivationFunctionType as AF, AxisListType
 
 RO, ST, NCH = 2, 3, 3
+CUT0 = 72
 BS = {"float32": 4, "int32": 4, "bfloat16": 2, "float16": 2, "uint16": 2}
 SCRATCH, ALIAS, POOL = {}, {}, {}
 
@@ -17,11 +18,11 @@ def _s(names, cols, dtype):
 
 
 _b("X", 4112, "bfloat16"); _b("O", 4112, "int32"); _b("OX OT OE", 1024, "int32"); _b("NB", 512, "int32"); _b("YN EXS", 512, "float32")
-_b("XG0 XG1 XG2 NR0 NR1", 2048, "bfloat16"); _b("PO0 PO1 PO2 PO3", 128, "uint16"); _b("PF0 PF1 PF2 PF3 SEL0 SEL1 M0 IOH", 128, "float16")
+_b("XG0 XG1 XG2 NR0 NR1", 2048, "bfloat16"); _b("PO0 PO1 PO2 PO3", 128, "uint16"); _b("PF0 PF1 PF2 PF3 SEL0 SEL1 M0_0 M0_1 M0_2 IOH", 128, "float16")
 _b("D0 D1 D2 KEY MI EX0 EX1 PEN", 512, "float32", "psum"); _b("NO0 NO1", 128, "bfloat16")
 _b("S1_0 S1_1 S1_2", 384, "float32"); _b("SG0 SG1 SG2", 24 * 34, "bfloat16"); _b("XOH0 XOH1 YU", 24 * 128, "float16"); _b("HOH", 24 * 128, "bfloat16")
-_s("VMB0 VMB1 VMB2 QB0 QB1 QB2 LOB0 LOB1 LOB2 HP0 HP1 HP2 XC0 XC1 WL0 WL1 FA FB FC BB BC BD EF EG EH HM0 HM1 HM2 FC0 FC1 UM0 UM1 CF", 24, "float32")
-_s("VL IA IB IC LWI BI EA EB EC PA PB_ PC", 24, "int32"); _s("LW", 24, "uint16"); _s("MM PB I16", 8, "float32"); _s("QA QT", 24, "bfloat16")
+_s("VMB0 VMB1 VMB2 QB0 QB1 QB2 LOB0 LOB1 LOB2 HP0 HP1 HP2 XC0 XC1 WL0 WL1 FA0 FA FB BB BC BD EF EG EH HM0 HM1 HM2 FC0 FC1 UM0 UM1 CF", 24, "float32")
+_s("VL IA IB IC ID_ LWI BI EA EB EC PA PB_ PC", 24, "int32"); _s("LW", 24, "uint16"); _s("MM PB I16", 8, "float32"); _s("QA QT", 24, "bfloat16")
 for _r in range(RO):
     for _i in range(3):
         _b("Z%d_%d" % (_r, _i), 384, "bfloat16")
@@ -190,7 +191,7 @@ def rank_program(g, core, T, topo):
             arrives("aL%d_%d" % (r, s), A("LL%d_%d" % (r, s)), T.cores[(rank + s) % N])
         arrives("aU%d" % r, A("UL%d" % r), prv)
 
-    ms(A("X", 2048, 2049), 512.0); ms(A("O", 2048, 2049), 0)
+    ms(A("X", 2048, 2049), 512.0); ms(A("X", 4097, 4112), 512.0); ms(A("O", 2048, 2049), 0); ms(A("O", 4097, 4112), 0)
     dma("dnb", ap(A("NB")), T.nb[:, :], "Y", [], [A("NB")])
     dma("dv", ap(A("VL")), T.v[:, :], "S", [], [A("VL")])
     for i in range(4):
@@ -203,7 +204,6 @@ def rank_program(g, core, T, topo):
     iota(A("KB", p1=1), [[0, 8], [-1, 16]], 15, 0)
     iota(A("KF"), [[0, 8], [1, 16]], 0, 0)
     iota(A("GF"), [[1, 8], [0, 16]], 0, 0)
-    ms(A("X", 4097, 4112), 512.0); ms(A("O", 4097, 4112), 0)
     ms(A("ONE"), 1.0); ms(A("QROW", p1=1), -0.25); ms(A("PB", 4, 5), 524288.0)
     cp(A("CF", 0, 1), A("CI", 0, 1))
     ts(A("CI", 4, 5), A("CI", 0, 1), 15, OP.bitwise_and); cp(A("CF", 4, 5), A("CI", 4, 5))
@@ -237,12 +237,14 @@ def rank_program(g, core, T, topo):
             dma("dcp", ap(d), ap(src), "Y", [src], [d])
 
     def xg(n):
-        gather_s(A("XG%d" % (n % 3)), A("X"), A("PO%d" % (n % 4)))
+        x, po, c = "XG%d" % (n % 3), "PO%d" % (n % 4), 128 if n else CUT0
+        gather_s(A(x, 0, 16 * c), A("X"), A(po, 0, c))
+        if c < 128: gather_v(A(x, 16 * c, 2048), A("X"), A(po, c, 128))
 
     for q in range(8):
         src, d = A("OT", p0=16 * q, p1=16 * q + 16), A("OX", 128 * q, 128 * q + 128)
         dma("dox", ap(d), ap(src), "Y", [src], [d])
-    og(0, 0); xg(0); og(1, 0); xg(1); copies()
+    og(0, 0); og(1, 0); xg(0); xg(1); copies()
     ts(A("DB"), A("IOT"), A("CF", 12, 13), OP.is_equal)
     ts(A("WU"), A("I16"), A("CF", 8, 9), OP.is_equal, A("CF", 16, 17), OP.mult)
     ts(A("DUB"), A("IOT"), A("CF", 12, 13), OP.is_equal, A("CF", 16, 17), OP.mult)
@@ -311,19 +313,21 @@ def rank_program(g, core, T, topo):
                     send(T.cores[(rank - s) % N], A("LL%d_%d" % (r, s)), A("LU%d_%d" % (r, s)), "aL%d_%d" % (r, s))
 
         def codes():
-            for i in range(3):
-                mm(A("MI", 256 + 8 * i, 264 + 8 * i), A("Z%d_0" % r, 128 * i, 128 * i + 128), A("WU"), True, True)
-            cp(A("IA"), A("MI", 256, 280)); ts(A("FA"), A("VL"), -2048.0, OP.add); ts(A("IB"), A("IA"), 4095, OP.bitwise_and)
-            for b in range(16):
-                mm(A("MI", 288, 312), A("DUB", 15 - b, 143 - b), A("Z%d_0" % r, b, 384, 16), b == 0, b == 15)
-            tt(A("IA"), A("MI", 288, 312), A("VL"), OP.add)
-            ts(A("FB"), A("IB"), 2048.0, OP.is_gt, -4096.0, OP.mult); ts(A("IC"), A("IA"), 4095, OP.bitwise_and)
-            tt(A("UV%d" % r, 24, 48), A("IB"), A("FB"), OP.add)
-            for i in range(3):
-                for a in range(8):
-                    ts(A("M0", 16 * a, 16 * a + 16), A("BM"), A("FA", 8 * i + a, 8 * i + a + 1), OP.mult)
-                mm(A("MI", 320 + 8 * i, 328 + 8 * i), A("M0"), A("B8"), True, True)
-            cp(A("VMB0"), A("MI", 320, 344))
+            def products():
+                for i in range(3):
+                    mm(A("MI", 256 + 8 * i, 264 + 8 * i), A("Z%d_0" % r, 128 * i, 128 * i + 128), A("WU"), True, True)
+                for b in range(16):
+                    mm(A("MI", 288, 312), A("DUB", 15 - b, 143 - b), A("Z%d_0" % r, b, 384, 16), b == 0, b == 15)
+                ts(A("FA0"), A("VL"), -2048.0, OP.add)
+
+            def spread(i, a):
+                ts(A("M0_%d" % i, 16 * a, 16 * a + 16), A("BM"), A("FA0", 8 * i + a, 8 * i + a + 1), OP.mult)
+                if a == 7: mm(A("MI", 320 + 8 * i, 328 + 8 * i), A("M0_%d" % i), A("B8"), True, True)
+            m = [lambda i=i, a=a: spread(i, a) for i in range(3) for a in range(8)]
+            u = [lambda: cp(A("IA"), A("MI", 256, 280)), lambda: tt(A("ID_"), A("MI", 288, 312), A("VL"), OP.add), lambda: ts(A("IB"), A("IA"), 4095, OP.bitwise_and),
+                 lambda: ts(A("IC"), A("ID_"), 4095, OP.bitwise_and),
+                 lambda: ts(A("FB"), A("IB"), 2048.0, OP.is_gt, -4096.0, OP.mult), lambda: tt(A("UV%d" % r, 24, 48), A("IB"), A("FB"), OP.add)]
+            return [products] + m[:8] + weave(u, m[8:]) + [lambda: cp(A("VMB0"), A("MI", 320, 344))]
 
         def exdig(s):
             v = A("VMB0") if s == 0 else A("UL%d" % r, 0, 24)
@@ -376,16 +380,15 @@ def rank_program(g, core, T, topo):
                 cp(A("AC"), A("AR"))
                 for i in range(3): mm(A("MI", 352, 353, p1=8), A("QT", 8 * i, 8 * i + 8), A("ONE", 0, 1), i == 0, False)
                 mm(A("MI", 352, 353, p1=8), A("B8B"), A("AC"), False, True)
-                cp(A("AI", p1=8), A("MI", 352, 353, p1=8))
 
             def m2():
                 cp(A("AB", p1=8), A("AJ", p1=8))
                 mm(A("MI", 360, 361), A("REP", p1=8), A("AB", p1=8), True, True)
-                ts(A("FCOL"), A("MI", 360, 361), -0.0625 / 64, OP.mult, 1.5625 / 64, OP.add)
             return [lambda: ts(A("QA"), A("GO%d_0" % r), -1.0, OP.mult, 1.0, OP.add), alive(1), alive(2),
                 lambda: tt(A("QT"), A("QA"), A("GO%d_1" % r), OP.subtract),
                 lambda: run("V", [A("AL")], [A("AR")], lambda: g.vector.tensor_reduce(ap(A("AR")), ap(A("AL")), AxisListType.X, OP.add)),
-                m1, lambda: ts(A("AJ", p1=8), A("AI", p1=8), 3, OP.bitwise_and), m2]
+                m1], [lambda: cp(A("AI", p1=8), A("MI", 352, 353, p1=8)), lambda: ts(A("AJ", p1=8), A("AI", p1=8), 3, OP.bitwise_and), m2], [
+                lambda: ts(A("FCOL"), A("MI", 360, 361), -0.0625 / 64, OP.mult, 1.5625 / 64, OP.add)]
 
         def boats():
             o = [lambda: cp(A("FA"), A("IC"))]
@@ -410,15 +413,19 @@ def rank_program(g, core, T, topo):
                 act(zn, y, AF.Copy)
                 if last: dma("oyv", T.yz[:, :], ap(zn), "Y", [zn], [])
 
-        if r: og(1, r); xg(1)
-        codes()
+        fq.extend(codes())
         for n in range(9):
             s, i = divmod(n, 3)
             if i == 0 and n:
+                if n == 3: tick(999)
                 pa(n - 1, 0); tick(2); pa(n - 1, 1); tick(2); pa(n - 1, 2); tick(4); pb(n - 1); tick(8); pc(n - 1)
                 og(n + 1, r); xg(n + 1)
                 e, x = exdig(s - 1)
-                fq.extend(weave(e, pendig(s - 1, 0, 24)) + (weave(x, settle()) if s == 2 and not last else x))
+                fq.extend(weave(e, pendig(s - 1, 0, 24)))
+                if s == 2 and not last:
+                    c0, c1, c2 = settle()
+                    x = weave(x[:6], c0) + x[6:16] + weave(x[16:19], c1) + x[19:] + c2
+                fq.extend(x)
             sub(n, 0); sub(n, 1); sub(n, 2)
             if i == 0 and n: tick(8)
             if n == 7:
@@ -438,7 +445,7 @@ def rank_program(g, core, T, topo):
                 if b == 2:
                     if i == 0: og(n + 2, r); xg(n + 2)
                     if i == 2 and n < 8: og(n + 1, r); xg(n + 1)
-                tick(2)
+                tick(3)
             if n in (3, 5, 6): own((3, 5, 6).index(n))
         e, x = penmask(2, 0, 16, False, False)
         fq.extend(pendig(2, 0, 16) + e + x)
@@ -451,7 +458,7 @@ def rank_program(g, core, T, topo):
         tt(A("HC", 0, 263), A("HC0", 1, 264), A("HC0", 0, 263), OP.is_gt)
         for q in range(8):
             src, d = A("HC", 33 * q, 33 * q + 32), A("HS", p0=q, p1=q + 1)
-            dma("dhs", ap(d), ap(src), "Y", [src], [d])
+            dma("dhs", ap(d), ap(src), "YS"[q % 2], [src], [d])
         tick(999)
         fq.extend(boats())
         for h in range(2):
@@ -461,17 +468,17 @@ def rank_program(g, core, T, topo):
             for q in range(4 * h, 4 * h + 4):
                 src, d = A("OX" if last else "OE", 128 * q, 128 * q + 128), A("O", 0, 1024, p0=16 * q, p1=16 * q + 16)
                 dma("dex", ap(d), ap(src), "Y", [src], [d])
-        tick(999)
         for c in range(8):
             d = A("D%d" % (c % 3)); x = A("X", 512 * c + c // 4, 512 * c + c // 4 + 512)
             mm(d, A("ID"), x, True, False); mm(d, A("NREP", p1=8), A("HS", 512 * c, 512 * c + 512, p1=8), False, True)
-            if c % 2: ts(x, d, 0.0, OP.max)
+            if c in (3, 5, 7): tick(3); ts(x, d, 0.0, OP.max)
             else: act(x, d, AF.Relu)
             if last: dma("oyx%d" % (c % 2), T.yx[:, 512 * c:512 * c + 512], ap(x), "Y", [x], [])
+        tick(999)
         if last:
             ts(A("EXS"), A("O", 512, 1024), 4096.0, OP.mult); tt(A("YN"), A("EXS"), A("O", 0, 512), OP.add)
             dma("oyn", T.yn[:, :], ap(A("YN")), "Y", [A("YN")], [])
-        else: og(0, r + 1); xg(0); copies()
+        else: og(0, r + 1); og(1, r + 1); xg(0); xg(1); copies()
 
     for r in range(RO):
         round_(r)

from concourse.mybir import dt, AluOpType as OP, ActivationFunctionType as AF, AxisListType

RO, ST, NCH = 2, 3, 3
CUT0 = 72
BS = {"float32": 4, "int32": 4, "bfloat16": 2, "float16": 2, "uint16": 2}
SCRATCH, ALIAS, POOL = {}, {}, {}


def _b(names, cols, dtype, where="sbuf"):
    for n in names.split():
        SCRATCH[n] = (where, [128, cols], dtype)


def _s(names, cols, dtype):
    for n in names.split():
        w = 32 // BS[dtype]; o = POOL.get(dtype, 0)
        ALIAS[n] = ("pool_" + dtype, o, cols); POOL[dtype] = o + (cols + w - 1) // w * w


_b("X", 4112, "bfloat16"); _b("O", 4112, "int32"); _b("OX OT OE", 1024, "int32"); _b("NB", 512, "int32"); _b("YN EXS", 512, "float32")
_b("XG0 XG1 XG2 NR0 NR1", 2048, "bfloat16"); _b("PO0 PO1 PO2 PO3", 128, "uint16"); _b("PF0 PF1 PF2 PF3 SEL0 SEL1 M0_0 M0_1 M0_2 IOH", 128, "float16")
_b("D0 D1 D2 KEY MI EX0 EX1 PEN", 512, "float32", "psum"); _b("NO0 NO1", 128, "bfloat16")
_b("S1_0 S1_1 S1_2", 384, "float32"); _b("SG0 SG1 SG2", 24 * 34, "bfloat16"); _b("XOH0 XOH1 YU", 24 * 128, "float16"); _b("HOH", 24 * 128, "bfloat16")
_s("VMB0 VMB1 VMB2 QB0 QB1 QB2 LOB0 LOB1 LOB2 HP0 HP1 HP2 XC0 XC1 WL0 WL1 FA0 FA FB BB BC BD EF EG EH HM0 HM1 HM2 FC0 FC1 UM0 UM1 CF", 24, "float32")
_s("VL IA IB IC ID_ LWI BI EA EB EC PA PB_ PC", 24, "int32"); _s("LW", 24, "uint16"); _s("MM PB I16", 8, "float32"); _s("QA QT", 24, "bfloat16")
for _r in range(RO):
    for _i in range(3):
        _b("Z%d_%d" % (_r, _i), 384, "bfloat16")
        _s("GO%d_%d" % (_r, _i), 24, "float32"); _s("LU%d_%d" % (_r, _i), 24, "uint16")
        if _i < 2:
            _s("F%d_%d" % (_r, _i), 24, "float32"); _b("ZO%d_%d" % (_r, _i), 384, "bfloat16")
        if _i > 0:
            _s("FL%d_%d GL%d_%d" % (_r, _i, _r, _i), 24, "float32"); _s("LV%d_%d LL%d_%d" % (_r, _i, _r, _i), 24, "uint16")
    _s("UV%d UL%d" % (_r, _r), 48, "float32")
_b("HC0", 264, "float32"); _b("HC", 264, "bfloat16"); _b("HS", 4096, "bfloat16")
_b("RY", 384, "float32"); _b("RB RN RE RD ONE", 384, "bfloat16")
_b("IOT", 144, "float32"); _b("IOB ID HID NID FI NFI REP NREP KB QROW", 128, "bfloat16"); _s("CI", 8, "int32")
_s("W8 WU B8B", 8, "bfloat16"); _s("B8", 8, "float16"); _s("BM", 16, "float16"); _b("DB", 144, "float16"); _b("DUB", 144, "bfloat16")
_b("RST KF GF", 128, "float32"); _b("ZR", 512, "float16")
_s("AL", 48, "float32"); _s("AR FCOL", 1, "float32"); _s("AC AB", 1, "bfloat16"); _s("AI AJ", 1, "int32")
for _d in POOL:
    _b("pool_" + _d, POOL[_d], _d)

SEMAPHORES = ["V", "S", "P", "G", "ls", "dnb", "dv", "dz", "dx0", "dx1", "dx2", "dx3", "dhs", "dex", "dox", "dcp", "oyx0", "oyx1", "oyn", "oyv"]
for _r in range(RO):
    for _j in (1, 2):
        for _i in range(NCH):
            SEMAPHORES += ["aF%d_%d_%d" % (_r, _j, _i), "aV%d_%d_%d" % (_r, _j, _i), "aZ%d_%d_%d" % (_r, _j, _i)]
        SEMAPHORES += ["aG%d_%d" % (_r, _j), "aL%d_%d" % (_r, _j)]
    SEMAPHORES += ["aU%d" % _r]

MAG = 12582912.0
M16 = 201326592.0
UP, DOWN, EPS = 4097 / 4096, 4095 / 4096, 0.00015
THR0 = 16.0 * (34816 + 1) - 0.5


def rank_program(g, core, T, topo):
    rank = T.rank_of(core)
    if rank is None:
        return
    N = len(T.cores)
    nxt, prv = T.cores[(rank + 1) % N], T.cores[(rank - 1) % N]
    eng = {"V": g.vector, "S": g.scalar, "P": g.tensor, "G": g, "Y": g.sync}
    cnt, snap, acc, known = {}, {}, {}, {q: {} for q in eng}

    def A(name, c0=0, c1=None, step=1, p0=0, p1=128):
        if name in ALIAS:
            n, o, w = ALIAS[name]
            return (n, o + c0, o + (w if c1 is None else c1), step, p0, p1)
        return (name, c0, SCRATCH[name][1][1] if c1 is None else c1, step, p0, p1)

    def ap(a):
        t = T[a[0]]
        return t[a[4]:a[5], a[1]:a[2]] if a[3] == 1 else t[a[4]:a[5], a[1]:a[2]:a[3]]

    def span(a):
        w = BS[SCRATCH[a[0]][2]]
        if SCRATCH[a[0]][0] == "psum": return (0, 128, 0, 2048)
        return (a[4], a[5], a[1] * w, a[2] * w)

    def learn(q, comp, n):
        k = known[q]
        if k.get(comp, 0) >= n: return
        k[comp] = n
        for c2, n2 in snap.get((comp, n), {}).items():
            if k.get(c2, 0) < n2: k[c2] = n2

    def hazards(q, comp, reads, writes):
        need = {}
        for lst, w in ((reads, False), (writes, True)):
            for a in lst:
                ps = SCRATCH[a[0]][0] == "psum"; s = span(a)
                for (t, ow, oc, on, oq) in acc.get(a[0], []):
                    b = 16 if ow and w and (oc in eng) != (comp in eng) else 1
                    if not (s[0] < t[1] and t[0] < s[1] and s[2] // b * b < -(-t[3] // b) * b and t[2] // b * b < -(-s[3] // b) * b): continue
                    if ps:
                        if oq == q and oc == comp and (q == "P" or not (ow or w)): continue
                    elif not (ow or w): continue
                    if oc[0] in "do" and known[q].get(oc, 0) < on: on = cnt[oc]
                    if need.get(oc, 0) < on: need[oc] = on
        for oc in sorted(need, key=lambda c: -need[c]):
            if known[q].get(oc, 0) < need[oc]:
                eng[q].wait_ge(T.sem[oc], need[oc]); learn(q, oc, need[oc])

    def note(q, comp, n, reads, writes):
        for a in writes:
            s = span(a); ps = SCRATCH[a[0]][0] == "psum"
            if not ps: acc[a[0]] = [r for r in acc.get(a[0], []) if not (s[0] <= r[0][0] and r[0][1] <= s[1] and s[2] <= r[0][2] and r[0][3] <= s[3])]
        for lst, w in ((reads, False), (writes, True)):
            for a in lst:
                s = span(a)
                l = [r for r in acc.setdefault(a[0], []) if not (r[0] == s and r[1] == w and r[2] == comp and r[4] == q)]
                acc[a[0]] = l + [(s, w, comp, n, q)]

    def run(q, reads, writes, call):
        hazards(q, q, reads, writes)
        i = call(); cnt[q] = cnt.get(q, 0) + 1
        i.then_inc(T.sem[q], 1)
        snap[(q, cnt[q])] = dict(known[q])
        note(q, q, cnt[q], reads, writes)

    def dma(sem, out, in_, q="Y", reads=(), writes=()):
        hazards(q, sem, reads, writes)
        eng[q].dma_start(out, in_).then_inc(T.sem[sem], 16)
        cnt[sem] = cnt.get(sem, 0) + 16
        snap[(sem, cnt[sem])] = dict(known[q])
        note(q, sem, cnt[sem], reads, writes)

    def send(dst, out, in_, sem):
        hazards("G", "ls", [in_], [])
        rid, pid, _ = topo.addr(dst)
        g.remote_dma(ap(out), ap(in_), T.sem[sem], T.sem["ls"], pid, rid, topo.mask(core, dst))
        cnt["ls"] = cnt.get("ls", 0) + len(topo.engines(core, dst))

    def arrives(sem, a, src):
        cnt[sem] = len(topo.engines(src, core)); note("R", sem, cnt[sem], [], [a])

    def col(x):
        return (ap(x), [x]) if isinstance(x, tuple) else (x, [])

    def ts(out, in0, s1, op0, s2=None, op1=None):
        v1, r1 = col(s1); v2, r2 = col(s2)
        if op1 is None: run("V", [in0] + r1, [out], lambda: g.vector.tensor_scalar(ap(out), ap(in0), v1, None, op0))
        else: run("V", [in0] + r1 + r2, [out], lambda: g.vector.tensor_scalar(ap(out), ap(in0), v1, v2, op0, op1))

    def tt(out, a, b, op):
        run("V", [a, b], [out], lambda: g.vector.tensor_tensor(ap(out), ap(a), ap(b), op))

    def cp(out, a):
        run("V", [a], [out], lambda: g.vector.tensor_copy(ap(out), ap(a)))

    def ms(out, c):
        run("V", [], [out], lambda: g.vector.memset(ap(out), c))

    def mm(out, l, r, start, stop):
        run("P", [l, r], [out], lambda: g.tensor.matmul(ap(out), ap(l), ap(r), start, stop))

    def act(out, a, f, bias=None):
        v, r = col(bias)
        if bias is None: run("S", [a], [out], lambda: g.scalar.activation(ap(out), ap(a), f))
        else: run("S", [a] + r, [out], lambda: g.scalar.activation(ap(out), ap(a), f, bias=v))

    def gather_v(out, win, off):
        run("V", [win, off], [out], lambda: g.vector.tensor_copy(ap(out), ap(win).indirect(ap(off))))

    def gather_s(out, win, off):
        run("S", [win, off], [out], lambda: g.scalar.activation(ap(out), ap(win).indirect(ap(off)), AF.Copy))

    def iota(out, pat, base, cm, flag=True):
        if flag: run("G", [], [out], lambda: g.iota(ap(out), pat, base, cm, allow_small_or_imprecise_dtypes=True))
        else: run("G", [], [out], lambda: g.iota(ap(out), pat, base, cm))

    fq = []

    def tick(k=1):
        while fq and k: fq.pop(0)(); k -= 1

    def weave(a, b):
        o = []
        for i in range(max(len(a), len(b))): o += a[i:i + 1] + b[i:i + 1]
        return o

    for r in range(RO):
        for s in (1, 2):
            for i in range(NCH):
                arrives("aF%d_%d_%d" % (r, s, i), A("FL%d_%d" % (r, s), 8 * i, 8 * i + 8), prv)
                arrives("aV%d_%d_%d" % (r, s, i), A("LV%d_%d" % (r, s), 8 * i, 8 * i + 8), prv)
                arrives("aZ%d_%d_%d" % (r, s, i), A("Z%d_%d" % (r, s), 128 * i, 128 * i + 128), prv)
            arrives("aG%d_%d" % (r, s), A("GL%d_%d" % (r, s)), nxt)
            arrives("aL%d_%d" % (r, s), A("LL%d_%d" % (r, s)), T.cores[(rank + s) % N])
        arrives("aU%d" % r, A("UL%d" % r), prv)

    ms(A("X", 2048, 2049), 512.0); ms(A("X", 4097, 4112), 512.0); ms(A("O", 2048, 2049), 0); ms(A("O", 4097, 4112), 0)
    dma("dnb", ap(A("NB")), T.nb[:, :], "Y", [], [A("NB")])
    dma("dv", ap(A("VL")), T.v[:, :], "S", [], [A("VL")])
    for i in range(4):
        a = A("X", 1024 * i + i // 2, 1024 * i + i // 2 + 1024)
        dma("dx%d" % i, ap(a), T.tracks[:, 1024 * i:1024 * i + 1024], "YS"[i % 2], [], [a])
    dma("dz", ap(A("Z0_0")), T.z[:, :], "Y", [], [A("Z0_0")])
    iota(A("CI", 0, 1), [[1, 1]], 0, 1, False)
    iota(A("IOT"), [[1, 144]], 0, 0)
    iota(A("I16"), [[16, 8]], 0, 0)
    iota(A("KB", p1=1), [[0, 8], [-1, 16]], 15, 0)
    iota(A("KF"), [[0, 8], [1, 16]], 0, 0)
    iota(A("GF"), [[1, 8], [0, 16]], 0, 0)
    ms(A("ONE"), 1.0); ms(A("QROW", p1=1), -0.25); ms(A("PB", 4, 5), 524288.0)
    cp(A("CF", 0, 1), A("CI", 0, 1))
    ts(A("CI", 4, 5), A("CI", 0, 1), 15, OP.bitwise_and); cp(A("CF", 4, 5), A("CI", 4, 5))
    ts(A("ID"), A("IOT", 0, 128), A("CF", 0, 1), OP.is_equal)
    tt(A("CF", 8, 9), A("CF", 0, 1), A("CF", 4, 5), OP.subtract)
    ts(A("FI"), A("ID"), 1.5625 / 64, OP.mult); ts(A("NFI"), A("ID"), -1.5625 / 64, OP.mult)
    ts(A("CF", 12, 13), A("CF", 8, 9), 15.0, OP.add)
    ts(A("CF", 16, 17), A("CF", 4, 5), 2.0, OP.mult, 1.0, OP.add)
    for b in range(4):
        ts(A("CI", 1, 2), A("CI", 4, 5), b, OP.arith_shift_right, 1, OP.bitwise_and)
        ts(A("PB", 0, 1), A("CI", 1, 2), 2.0 ** -(1 << b) - 1.0, OP.mult, 1.0, OP.add)
        tt(A("PB", 4, 5), A("PB", 4, 5), A("PB", 0, 1), OP.mult)
    ts(A("W8"), A("I16"), A("CF", 8, 9), OP.is_equal, A("PB", 4, 5), OP.mult)
    ts(A("RST"), A("KF"), 0.0, OP.is_equal, -4194304.0, OP.mult)
    ts(A("LWI"), A("VL"), 1023, OP.bitwise_and)
    ts(A("B8"), A("I16"), A("CF", 8, 9), OP.is_equal)
    cp(A("LW"), A("LWI"))
    ts(A("BM"), A("IOT", 0, 16), A("CF", 4, 5), OP.is_equal)
    ts(A("OT", 0, 512), A("NB"), 4095, OP.bitwise_and); ts(A("OT", 512, 1024), A("NB"), 12, OP.arith_shift_right)
    ts(A("O", 0, 512), A("OT", 0, 512), UP, OP.mult, EPS, OP.add); ts(A("O", 512, 1024), A("OT", 512, 1024), UP, OP.mult, EPS, OP.add)

    def og(n, r):
        s, i = divmod(n, 3)
        po = A("PO%d" % (n % 4)); l = A("LV%d_%d" % (r, s), 8 * i, 8 * i + 8) if s else A("LW", 8 * i, 8 * i + 8)
        gather_v(po, A("O", 0, 4112) if s else A("O", 0, 1024), l); tick()
        ts(A("PF%d" % (n % 4)), po, -2048.0, OP.add)

    def copies():
        for a in (1024, 2049, 3073):
            src, d = A("O", 0, 1024), A("O", a, a + 1024)
            dma("dcp", ap(d), ap(src), "Y", [src], [d])

    def xg(n):
        x, po, c = "XG%d" % (n % 3), "PO%d" % (n % 4), 128 if n else CUT0
        gather_s(A(x, 0, 16 * c), A("X"), A(po, 0, c))
        if c < 128: gather_v(A(x, 16 * c, 2048), A("X"), A(po, c, 128))

    for q in range(8):
        src, d = A("OT", p0=16 * q, p1=16 * q + 16), A("OX", 128 * q, 128 * q + 128)
        dma("dox", ap(d), ap(src), "Y", [src], [d])
    og(0, 0); og(1, 0); xg(0); xg(1); copies()
    ts(A("DB"), A("IOT"), A("CF", 12, 13), OP.is_equal)
    ts(A("WU"), A("I16"), A("CF", 8, 9), OP.is_equal, A("CF", 16, 17), OP.mult)
    ts(A("DUB"), A("IOT"), A("CF", 12, 13), OP.is_equal, A("CF", 16, 17), OP.mult)
    ts(A("HID"), A("ID"), 0.5, OP.mult); ts(A("NID"), A("ID"), -1.0, OP.mult)
    ts(A("REP", p1=8), A("GF", p1=8), A("CF", 0, 1, p1=8), OP.is_equal)
    ts(A("B8B"), A("I16"), A("CF", 8, 9), OP.is_equal)
    cp(A("IOH"), A("IOT", 0, 128)); ts(A("IOB"), A("IOT", 0, 128), 1.0, OP.add)
    ts(A("NREP", p1=8), A("REP", p1=8), -45.0, OP.mult)
    ts(A("ZR", p1=1), A("O", 0, 512, p1=1), 0.0, OP.mult)

    def round_(r):
        last = r == RO - 1

        def sub(n, b):
            s, i = divmod(n, 3); d = "D%d" % ((4 * n + b) % 3); z = A("Z%d_%d" % (r, s), 128 * i, 128 * i + 128)
            for j in range(4):
                o = A(d, 128 * j, 128 * j + 128)
                mm(o, A("FI"), A("XG%d" % (n % 3), 4 * b + j, 2048, 16), True, False); mm(o, A("NFI"), z, False, True)

        def near(n, b, h):
            ts(A("NR%d" % (n % 2), 512 * b + 256 * h, 512 * b + 256 * h + 256), A("D%d" % ((4 * n + b) % 3), 256 * h, 256 * h + 256), MAG, OP.add, MAG, OP.is_equal)

        def tm(n, b):
            if b == 0: mm(A("KEY", 0, 128), A("ONE", 0, 128, p1=1), A("KB", p1=1), True, False)
            for k in range(4 * b, 4 * b + 4):
                mm(A("KEY", k, 128, 16), A("NR%d" % (n % 2), 128 * k, 128 * k + 128), A("W8"), False, k == 15)

        def pa(n, step):
            s, i = divmod(n, 3); s1 = A("S1_%d" % s, 128 * i, 128 * i + 128); m = A("S1_%d" % s, 128 * i + 15, 128 * i + 128, 16)
            if step == 0: run("V", [A("RST"), A("KEY", 0, 128)], [s1], lambda: g.vector.tensor_tensor_scan(ap(s1), ap(A("RST")), ap(A("KEY", 0, 128)), 0.0, OP.add, OP.max))
            elif step == 1:
                if s == 0: ts(A("MM"), m, THR0, OP.max)
                else: tt(A("MM"), m, A("FL%d_%d" % (r, s), 8 * i, 8 * i + 8), OP.max)
            else:
                for q in range(8):
                    ts(A("NO%d" % (n % 2), 16 * q, 16 * q + 16), A("KEY", 16 * q, 16 * q + 16), A("MM", q, q + 1), OP.is_ge)
                mm(A("MI", 0, 128), A("NO%d" % (n % 2)), A("ID"), True, True)

        def pb(n):
            s, i = divmod(n, 3); sl = "SEL%d" % (n % 2); m = A("S1_%d" % s, 128 * i + 15, 128 * i + 128, 16)
            tt(A(sl), A("MI", 0, 128), A("PF%d" % (n % 4)), OP.mult)
            for b in range(16):
                mm(A("MI", 128, 136), A("DB", 15 - b, 143 - b), A(sl, b, 128, 16), b == 0, b == 15)
            mm(A("MI", 136, 144), A(sl), A("B8"), True, True)
            ts(A("QB%d" % s, 8 * i, 8 * i + 8), m, -7.5, OP.add, M16, OP.add)
            go = A("GO%d_%d" % (r, s), 8 * i, 8 * i + 8)
            if s == 0: ts(go, m, THR0, OP.is_gt)
            else: tt(go, m, A("FL%d_%d" % (r, s), 8 * i, 8 * i + 8), OP.is_gt)
            if s < 2: ts(A("F%d_%d" % (r, s), 8 * i, 8 * i + 8), A("QB%d" % s, 8 * i, 8 * i + 8), M16, OP.subtract, 15.5, OP.add)

        def pc(n):
            s, i = divmod(n, 3); c = (8 * i, 8 * i + 8)
            lu = A("LU%d_%d" % (r, s), *c)
            ts(lu, A("MI", 128, 136), 2048.0, OP.add)
            if s < 2: send(nxt, A("LV%d_%d" % (r, s + 1), *c), lu, "aV%d_%d_%d" % (r, s + 1, i))
            act(A("UV%d" % r, *c) if s == 0 else A("VMB%d" % s, *c), A("MI", 136, 144), AF.Copy)
            if s < 2:
                send(nxt, A("FL%d_%d" % (r, s + 1), *c), A("F%d_%d" % (r, s), *c), "aF%d_%d_%d" % (r, s + 1, i))
                zo = A("ZO%d_%d" % (r, s), 128 * i, 128 * i + 128)
                gather_s(zo, A("X"), lu)
                send(nxt, A("Z%d_%d" % (r, s + 1), 128 * i, 128 * i + 128), zo, "aZ%d_%d_%d" % (r, s + 1, i))
            if i == 2:
                if s == 0: send(nxt, A("UL%d" % r), A("UV%d" % r), "aU%d" % r)
                else:
                    send(prv, A("GL%d_%d" % (r, s)), A("GO%d_%d" % (r, s)), "aG%d_%d" % (r, s))
                    send(T.cores[(rank - s) % N], A("LL%d_%d" % (r, s)), A("LU%d_%d" % (r, s)), "aL%d_%d" % (r, s))

        def codes():
            def products():
                for i in range(3):
                    mm(A("MI", 256 + 8 * i, 264 + 8 * i), A("Z%d_0" % r, 128 * i, 128 * i + 128), A("WU"), True, True)
                for b in range(16):
                    mm(A("MI", 288, 312), A("DUB", 15 - b, 143 - b), A("Z%d_0" % r, b, 384, 16), b == 0, b == 15)
                ts(A("FA0"), A("VL"), -2048.0, OP.add)

            def spread(i, a):
                ts(A("M0_%d" % i, 16 * a, 16 * a + 16), A("BM"), A("FA0", 8 * i + a, 8 * i + a + 1), OP.mult)
                if a == 7: mm(A("MI", 320 + 8 * i, 328 + 8 * i), A("M0_%d" % i), A("B8"), True, True)
            m = [lambda i=i, a=a: spread(i, a) for i in range(3) for a in range(8)]
            u = [lambda: cp(A("IA"), A("MI", 256, 280)), lambda: tt(A("ID_"), A("MI", 288, 312), A("VL"), OP.add), lambda: ts(A("IB"), A("IA"), 4095, OP.bitwise_and),
                 lambda: ts(A("IC"), A("ID_"), 4095, OP.bitwise_and),
                 lambda: ts(A("FB"), A("IB"), 2048.0, OP.is_gt, -4096.0, OP.mult), lambda: tt(A("UV%d" % r, 24, 48), A("IB"), A("FB"), OP.add)]
            return [products] + m[:8] + weave(u, m[8:]) + [lambda: cp(A("VMB0"), A("MI", 320, 344))]

        def exdig(s):
            v = A("VMB0") if s == 0 else A("UL%d" % r, 0, 24)

            def xoh(j): return lambda: ts(A("XOH%d" % s, 128 * j, 128 * j + 128), A("IOH"), A("XC%d" % s, j, j + 1), OP.is_equal)
            return [lambda: ts(A("EA"), v, 2048.0, OP.add, DOWN if s else 1.0, OP.mult), lambda: ts(A("EF"), A("QB%d" % s), M16, OP.subtract, 15.0, OP.add),
                    lambda: ts(A("EB"), A("EA"), 127, OP.bitwise_and), lambda: tt(A("EG"), A("EF"), A("S1_%d" % s, 15, 384, 16), OP.subtract),
                    lambda: cp(A("WL%d" % s), A("EB")), lambda: ts(A("EH"), A("EG"), 8.0, OP.mult),
                    lambda: ts(A("EC"), A("EA"), 7, OP.arith_shift_right, 7, OP.bitwise_and),
                    lambda: tt(A("XC%d" % s), A("EH"), A("EC"), OP.add)], [xoh(j) for j in range(24)]

        def exmask(s):
            def um():
                tt(A("UM%d" % s), A("UV%d" % r, 24, 48) if s == 0 else A("UL%d" % r, 24, 48), A("GL%d_%d" % (r, s + 1)), OP.mult)
                if s == 0:
                    for h in range(2): mm(A("EX%d" % h), A("ZR", 0, 128, p1=1), A("ZR", p1=1), True, False)

            def yu(j):
                q = j % 8; y = A("YU", 128 * j, 128 * j + 128)
                ts(y, A("IOH"), A("WL%d" % s, j, j + 1), OP.is_equal, A("UM%d" % s, j, j + 1), OP.mult)
                mm(A("EX%d" % (q // 4), q % 4 * 128, q % 4 * 128 + 128), A("XOH%d" % s, 128 * j, 128 * j + 128), y, False, s == 1 and j in (19, 23))
            return [um], [lambda j=j: yu(j) for j in range(24)]

        def pendig(s, c0, c1):
            v = A("UV%d" % r, c0, c1) if s == 0 else A("VMB%d" % s, c0, c1); a, b, c = A("PA", c0, c1), A("PB_", c0, c1), A("PC", c0, c1)

            def lob():
                ts(A("LOB%d" % s, c0, c1), b, -1.0, OP.mult, -0.5, OP.add)
                for j in range(c0, c1):
                    act(A("SG%d" % s, 34 * j, 34 * j + 33), A("IOT", 0, 33), AF.Sign, A("LOB%d" % s, j, j + 1))
            return [lambda: ts(a, v, 2048.0, OP.add, DOWN, OP.mult), lambda: ts(b, a, 31, OP.bitwise_and), lambda: ts(c, a, 5, OP.arith_shift_right),
                    lob, lambda: ts(A("HP%d" % s, c0, c1), c, 1.0, OP.add)]

        def penmask(s, c0, c1, first, end):
            m = A("HM%d" % s, c0, c1); hp = A("HP%d" % s, c0, c1); go = A("GO%d_%d" % (r, s), c0, c1)

            def hoh(j):
                q = j % 8; h = A("HOH", 128 * j, 128 * j + 128)
                if first and j == c0: mm(A("PEN", 0, 264), A("ZR", 0, 128, p1=1), A("ZR", 0, 264, p1=1), True, False)
                ts(h, A("IOB"), A("HM%d" % s, j, j + 1), OP.is_equal)
                mm(A("PEN", 33 * q, 33 * q + 33), h, A("SG%d" % s, 34 * j, 34 * j + 33), False, end and j == 23)
            if s < 2: pre = [lambda: tt(A("FC%d" % s, c0, c1), go, A("GL%d_%d" % (r, s + 1), c0, c1), OP.subtract), lambda: tt(m, hp, A("FC%d" % s, c0, c1), OP.mult)]
            else: pre = [lambda: tt(m, hp, go, OP.mult)]
            return pre, [lambda j=j: hoh(j) for j in range(c0, c1)]

        def settle():
            def alive(s): return lambda: ts(A("AL", 24 * s - 24, 24 * s), A("LV%d_%d" % (r, s)), 2048.0, OP.not_equal)

            def m1():
                cp(A("AC"), A("AR"))
                for i in range(3): mm(A("MI", 352, 353, p1=8), A("QT", 8 * i, 8 * i + 8), A("ONE", 0, 1), i == 0, False)
                mm(A("MI", 352, 353, p1=8), A("B8B"), A("AC"), False, True)

            def m2():
                cp(A("AB", p1=8), A("AJ", p1=8))
                mm(A("MI", 360, 361), A("REP", p1=8), A("AB", p1=8), True, True)
            return [lambda: ts(A("QA"), A("GO%d_0" % r), -1.0, OP.mult, 1.0, OP.add), alive(1), alive(2),
                lambda: tt(A("QT"), A("QA"), A("GO%d_1" % r), OP.subtract),
                lambda: run("V", [A("AL")], [A("AR")], lambda: g.vector.tensor_reduce(ap(A("AR")), ap(A("AL")), AxisListType.X, OP.add)),
                m1], [lambda: cp(A("AI", p1=8), A("MI", 352, 353, p1=8)), lambda: ts(A("AJ", p1=8), A("AI", p1=8), 3, OP.bitwise_and), m2], [
                lambda: ts(A("FCOL"), A("MI", 360, 361), -0.0625 / 64, OP.mult, 1.5625 / 64, OP.add)]

        def boats():
            o = [lambda: cp(A("FA"), A("IC"))]
            for lu in (A("LU%d_0" % r), A("LL%d_1" % r), A("LL%d_2" % r)):
                o += [lambda lu=lu: ts(A("BI"), lu, DOWN, OP.mult), lambda lu=lu: ts(A("BB"), lu, 2048.0, OP.is_equal), lambda: tt(A("BC"), A("FA"), A("BI"), OP.subtract),
                      lambda: tt(A("BD"), A("BC"), A("BB"), OP.mult), lambda: tt(A("FA"), A("BD"), A("BI"), OP.add)]
            if last: return o + [lambda: dma("oyv", T.yv[:, :], ap(A("FA")), "Y", [A("FA")], [])]
            return o + [lambda: cp(A("VL"), A("FA")), lambda: ts(A("LWI"), A("VL"), 1023, OP.bitwise_and), lambda: cp(A("LW"), A("LWI"))]

        z0, z1, zn, y = A("Z%d_0" % r), A("ZO%d_0" % r), A("Z%d_0" % (r + 1)) if not last else A("RD"), A("PEN", 0, 384)

        def own(part):
            if part == 0:
                mm(y, A("HID"), z0, True, False); mm(y, A("HID"), z1, False, False); mm(y, A("QROW", p1=1), A("ONE", p1=1), False, True)
                ts(A("RN"), z1, 256.0, OP.is_ge)
                act(A("RY"), y, AF.Copy, MAG); act(A("RB"), A("RY"), AF.Copy, -MAG)
            if part == 1:
                mm(y, A("ID"), z0, True, False); mm(y, A("NID"), A("RB"), False, True)
                tt(A("RE"), y, A("RN"), OP.mult)
            if part == 2:
                mm(y, A("ID"), A("RE"), True, False); mm(y, A("ID"), A("RB"), False, True)
                act(zn, y, AF.Copy)
                if last: dma("oyv", T.yz[:, :], ap(zn), "Y", [zn], [])

        fq.extend(codes())
        for n in range(9):
            s, i = divmod(n, 3)
            if i == 0 and n:
                if n == 3: tick(999)
                pa(n - 1, 0); tick(2); pa(n - 1, 1); tick(2); pa(n - 1, 2); tick(4); pb(n - 1); tick(8); pc(n - 1)
                og(n + 1, r); xg(n + 1)
                e, x = exdig(s - 1)
                fq.extend(weave(e, pendig(s - 1, 0, 24)))
                if s == 2 and not last:
                    c0, c1, c2 = settle()
                    x = weave(x[:6], c0) + x[6:16] + weave(x[16:19], c1) + x[19:] + c2
                fq.extend(x)
            sub(n, 0); sub(n, 1); sub(n, 2)
            if i == 0 and n: tick(8)
            if n == 7:
                e, x = penmask(0, 0, 24, True, False); e2, x2 = exmask(0)
                fq.extend(e[:1] + e2 + e[1:] + x + x2)
            for b in range(4):
                near(n, b, 0)
                if i and b == 0: pa(n - 1, 0)
                if i and b == 1: pa(n - 1, 2)
                near(n, b, 1)
                if b == 0: sub(n, 3)
                if i and b == 0: pa(n - 1, 1)
                if b == 1: tm(n, 0)
                if i and b == 1: tick(2); pb(n - 1)
                if i and b == 2: pc(n - 1)
                if b: tm(n, b)
                if b == 2:
                    if i == 0: og(n + 2, r); xg(n + 2)
                    if i == 2 and n < 8: og(n + 1, r); xg(n + 1)
                tick(3)
            if n in (3, 5, 6): own((3, 5, 6).index(n))
        e, x = penmask(2, 0, 16, False, False)
        fq.extend(pendig(2, 0, 16) + e + x)
        pa(8, 0); tick(2); pa(8, 1); tick(2); pa(8, 2); tick(5); pb(8); tick(8); pc(8)
        if not last: fq.extend([lambda: ts(A("FI"), A("ID"), A("FCOL"), OP.mult), lambda: ts(A("NFI"), A("ID"), A("FCOL"), OP.mult, -1.0, OP.mult)])
        d = pendig(2, 16, 24); e, x = penmask(2, 16, 24, False, False); e1, x1 = penmask(1, 0, 24, False, True); e2, x2 = exmask(1)
        tick(4); fq.extend(d); tick(10); fq.extend(e + x + e1[:1] + e2 + e1[1:] + x1); tick(999)
        act(A("HC0"), A("PEN", 0, 264), AF.Copy)
        fq.extend(x2); tick(8)
        tt(A("HC", 0, 263), A("HC0", 1, 264), A("HC0", 0, 263), OP.is_gt)
        for q in range(8):
            src, d = A("HC", 33 * q, 33 * q + 32), A("HS", p0=q, p1=q + 1)
            dma("dhs", ap(d), ap(src), "YS"[q % 2], [src], [d])
        tick(999)
        fq.extend(boats())
        for h in range(2):
            c = (512 * h, 512 * h + 512)
            tick(2); tt(A("OT", *c), A("EX%d" % h), A("OX", *c), OP.add); tick(1); ts(A("OX", *c), A("OT", *c), 4095, OP.bitwise_and)
            if not last: tick(1); ts(A("OE", *c), A("OX", *c), UP, OP.mult, EPS, OP.add)
            for q in range(4 * h, 4 * h + 4):
                src, d = A("OX" if last else "OE", 128 * q, 128 * q + 128), A("O", 0, 1024, p0=16 * q, p1=16 * q + 16)
                dma("dex", ap(d), ap(src), "Y", [src], [d])
        for c in range(8):
            d = A("D%d" % (c % 3)); x = A("X", 512 * c + c // 4, 512 * c + c // 4 + 512)
            mm(d, A("ID"), x, True, False); mm(d, A("NREP", p1=8), A("HS", 512 * c, 512 * c + 512, p1=8), False, True)
            if c in (3, 5, 7): tick(3); ts(x, d, 0.0, OP.max)
            else: act(x, d, AF.Relu)
            if last: dma("oyx%d" % (c % 2), T.yx[:, 512 * c:512 * c + 512], ap(x), "Y", [x], [])
        tick(999)
        if last:
            ts(A("EXS"), A("O", 512, 1024), 4096.0, OP.mult); tt(A("YN"), A("EXS"), A("O", 0, 512), OP.add)
            dma("oyn", T.yn[:, :], ap(A("YN")), "Y", [A("YN")], [])
        else: og(0, r + 1); og(1, r + 1); xg(0); xg(1); copies()

    for r in range(RO):
        round_(r)
    for sem in cnt:
        if known["G"].get(sem, 0) < cnt[sem]: g.wait_ge(T.sem[sem], cnt[sem])
